import numpy as np, ml_dtypes
CORES = [9,25,41,57]
N = 4
BF = ml_dtypes.bfloat16
def gentries(a):
    return np.ascontiguousarray(a.reshape(8, 16, -1).transpose(0, 2, 1)).reshape(8, -1)
def gtable(e):
    e = np.asarray(e); return np.ascontiguousarray(e.reshape(8, -1, 16).transpose(0, 2, 1)).reshape(128, -1).astype(np.int32)
C, F, P, CAP, L, T, RO = 2048, 4096, 256, 32, 3, 4, 3
def parts(rng):
    return dict(su=rng.integers(0, F, (N, 8, 16, C)), se=rng.integers(0, 2, (N, 8, 16, C)), pw=rng.integers(-7, 8, (N, 8, 16, F)), ot=rng.integers(0, C, (N, 8, L, F)),
                x=rng.integers(0, 16, (N, 8, 16, P)), dr=rng.integers(0, 16, (N, 8, 16, P)), c=rng.integers(0, C, (N, 8, P)),
                th=rng.choice(np.array([8, 9, 10, 10, 11, 11, 12, 17]), (N, 8, P)), hw=rng.integers(-7, 8, (N, 8, 16, 2)))
def pack(s):
    def b(a): return np.ascontiguousarray(a.reshape(N, 128, -1)).astype(np.float32).astype(BF)
    return {"sf": np.ascontiguousarray((2 * s["su"] + s["se"]).reshape(N, 128, C)).astype(np.int32), "pw": b(s["pw"]), "ot": np.ascontiguousarray(s["ot"].reshape(N, 8 * L, F)).astype(np.int32),
            "x0": b(s["x"]), "dr": b(s["dr"]), "c0": np.stack([gtable(a) for a in s["c"]]), "th": np.stack([gtable(a) for a in s["th"]]), "hw": b(s["hw"])}
def setup_inputs(rng):
    return pack(parts(rng))
def behind(rng, s, g):
    n = 2 * CAP; q = C // 4; e = np.arange(C)
    s["pw"][:, g] = rng.integers(1, 8, (N, 16, F)); s["x"][:, g] = rng.integers(1, 16, (N, 16, P))
    half = np.argsort(rng.random((N, 16, C)), axis=1) % 2
    s["se"][:, g] = np.where(e < q, 0, np.where(e < 2 * q, half, np.where(e < C - n, 1, 0)))
    s["ot"][:, g] = rng.integers(2 * q, C - n, (N, L, F)); s["c"][:, g] = rng.integers(0, q, (N, P)); s["th"][:, g] = rng.integers(0, 17, (N, P))
    o = np.stack([rng.permutation(P) for r in range(N)]); ask, late = o[:, :n], o[:, n:2 * n]
    for k in range(N):
        r = (k - 1) % N; y = s["x"][r, g][:, ask[r]]
        u = np.add.reduce(s["hw"][k, g][:, :, None] * y[:, None, :], axis=0); h = ((u[0] * u[1]) >> 5) & (F - 1)
        s["pw"][k, g][:, h] = np.array([1, -2] + [0] * 14)[:, None]
        s["ot"][k, g, 0, h] = rng.integers(q, 2 * q, n); s["ot"][k, g, 1, h] = rng.integers(0, q, n)
        free = np.setdiff1d(np.arange(F), h); mine = free[free % N == (k + 1) % N]
        s["su"][k, g] = rng.choice(free, (16, C)); b = rng.permutation(np.arange(2 * q, C - n))[:n]
        s["su"][k, g][:, b] = rng.choice(mine, (16, n))
        s["su"][k, g][:, C - n:] = h[rng.integers(0, n, (16, n))]; s["su"][k, g, 0, C - n:] = h
        s["c"][k, g, ask[k]] = b; s["th"][k, g, ask[k]] = rng.integers(1, 9, n)
        s["c"][k, g, late[k]] = C - n + np.arange(n); s["th"][k, g, late[k]] = rng.integers(9, 17, n)
    for k in range(N):
        s["x"][k, g, 0, late[k]] = 2 * T - 3; s["x"][k, g, 1, late[k]] = 0; s["dr"][k, g, 0, late[k]] = 0; s["dr"][k, g, 1, late[k]] = 1
def setup_inputs_room(rng):
    s = parts(rng); s["su"] = s["su"] - s["su"] % N + np.arange(C) % N
    for r in range(N):
        for g in range(0, 8, 2):
            n = rng.choice(np.array([0, 1, CAP - 1, CAP, CAP + 1, 2 * CAP]), N)
            if g == 0: n[(r + 1) % N] = CAP
            if g == 2: n[(r + 1) % N] = CAP + 1
            if g == 4: n[(r + 2) % N] = 2 * CAP
            k = np.full(P, -1); w = np.repeat(np.arange(N), n); k[:len(w)] = w; k = rng.permutation(k)
            s["c"][r, g] = rng.integers(0, C // N, P) * N + np.where(k < 0, rng.integers(0, N, P), k)
            s["th"][r, g] = np.where(k < 0, 0, 17)
    s["th"][:, 1] = 0
    s["th"][:, 3] = 17; s["pw"][:, 3] = rng.integers(1, 8, (N, 16, F)); s["se"][:, 3] = 0; s["x"][:, 3] = rng.integers(1, 16, (N, 16, P))
    for r in range(0, N, 2): s["c"][r, 3] = rng.integers(0, C // N, P) * N + (r + 1) % N
    s["pw"][:, 5] = rng.integers(5, 8, (N, 16, F)); s["se"][:, 5] = 1; s["x"][:, 5] = rng.integers(13, 16, (N, 16, P))
    s["th"][:, 5] = np.where(s["c"][:, 5] % N == N - 1, 0, rng.integers(1, 18, (N, P)))
    for p, e, k in ((0, 0, 0), (P - 1, C - 1, F - 1)):
        s["c"][:, 5, p] = e; s["th"][:, 5, p] = 17; s["su"][:, 5, :, e] = k
    behind(rng, s, 7)
    return pack(s)
def setup_inputs_ties(rng):
    s = parts(rng); five = rng.integers(0, F, (N, 8, 5, C))
    s["su"] = np.take_along_axis(five, rng.integers(0, 5, (N, 8, 16, C)), 2)
    s["pw"] = rng.integers(-1, 2, s["pw"].shape) * (rng.random(s["pw"].shape) < 0.4)
    s["x"] = rng.integers(0, 2, s["x"].shape); s["dr"] = rng.choice(np.array([0, 0, 1, 15]), s["dr"].shape)
    s["th"] = rng.integers(8, 18, (N, 8, P))
    for p, t in ((3, 17), (5, 16), (P - 1, 17)): s["x"][..., p] = 0; s["dr"][..., p] = 0; s["th"][..., p] = t
    return pack(s)
def turn(rng, s, g):
    h = C // 2
    s["pw"][:, g] = rng.integers(1, 8, (N, 16, F)); s["se"][:, g] = np.where(np.arange(C) < h, 1, 0)
    s["x"][:, g] = rng.integers(1, 16, (N, 16, P)); s["th"][:, g] = rng.integers(1, 17, (N, P))
    s["ot"][:, g, 0] = rng.integers(0, h, (N, F)); s["ot"][:, g, 1] = rng.integers(h, C, (N, F))
def setup_inputs_alike(rng):
    s = parts(rng); pool = rng.integers(0, F, (N, 8, 1, 12)); pool[..., 0] = 0; pool[..., 1] = F - 1
    s["su"] = np.take_along_axis(pool, rng.integers(0, 12, (N, 8, 16 * C))[:, :, None, :], 3).reshape(N, 8, 16, C)
    t = rng.integers(0, 8, P)
    for k in ("x", "dr", "c"): s[k][:, ::2] = s[k][:, ::2][..., t]
    h = C // 2; turn(rng, s, 1); turn(rng, s, 3)
    for r in range(N):
        k = np.full(P, 1); k[1 + rng.permutation(P - 2)[:int(rng.integers(65, 125))]] = 0; k[0] = 0; k[P - 1] = 2
        s["su"][r, 1, :, :h] = np.array([0, int(rng.integers(1, F - 1)), F - 1])[np.arange(h) % 3]
        s["c"][r, 1] = k + 3 * rng.integers(0, h // 3, P)
        o = rng.permutation(F)[:F // P * P].reshape(P, F // P); e = rng.permutation(h)[:P]
        s["su"][r, 3][:, e] = o[np.arange(P)[None, :], rng.integers(0, F // P, (16, P))]
        s["c"][r, 3] = e
    return pack(s)
def setup_inputs_ends(rng):
    s = parts(rng)
    s["su"] = np.where(rng.random(s["su"].shape) < 0.3, rng.choice(np.array([0, F - 1]), s["su"].shape), s["su"])
    s["ot"] = np.where(rng.random(s["ot"].shape) < 0.4, rng.choice(np.array([0, C - 1]), s["ot"].shape), s["ot"])
    s["c"] = np.where(rng.random(s["c"].shape) < 0.4, rng.choice(np.array([0, C - 1]), s["c"].shape), s["c"])
    s["pw"] = rng.choice(np.array([-7, 7]), s["pw"].shape)
    s["x"] = rng.choice(np.array([0, 15]), s["x"].shape); s["dr"] = rng.choice(np.array([0, 1, 15]), s["dr"].shape)
    s["th"] = rng.choice(np.array([0, 1, 8, 9, 10, 11, 16, 17]), s["th"].shape)
    s["hw"] = rng.choice(np.array([-7, 7]), s["hw"].shape); s["hw"][:, 0] = 7; s["hw"][:, 1, :, 0] = 7; s["hw"][:, 1, :, 1] = -7
    for p in (0, 7, P - 1): s["x"][..., p] = 15; s["dr"][..., p] = 0; s["th"][..., p] = 17
    return pack(s)
def setup_inputs_spread(rng):
    s = parts(rng)
    s["pw"] = np.rint(s["pw"] * rng.random((N, 8, 1, F))).astype(np.int64)
    s["x"] = (16 * rng.random((N, 8, 1, P)) * rng.random((N, 8, 16, P))).astype(np.int64)
    s["dr"] = (16 * rng.random((N, 8, 1, P)) * rng.random((N, 8, 16, P))).astype(np.int64)
    s["su"] = np.minimum((F * rng.random((N, 8, 16, C)) ** 3).astype(np.int64), F - 1)
    s["ot"] = np.minimum((C * rng.random((N, 8, L, F)) ** 2).astype(np.int64), C - 1)
    s["c"] = np.minimum((C * rng.random((N, 8, P)) ** 4).astype(np.int64), C - 1)
    s["th"] = rng.integers(0, 18, (N, 8, P))
    return pack(s)
def check_inputs(d):
    bad = []
    for k, lo, hi in (("sf", 0, 2 * F - 1), ("pw", -7, 7), ("ot", 0, C - 1), ("x0", 0, 15), ("dr", 0, 15), ("c0", 0, C - 1), ("th", 0, 17), ("hw", -7, 7)):
        a = np.asarray(d[k]).astype(np.float64)
        if not np.all((a >= lo) & (a <= hi) & (a == np.rint(a))): bad.append("range of " + k)
    return bad
def lowest(m, f):
    lane = np.broadcast_to(np.arange(P), m.shape); key = np.arange(N * 8).reshape(N, 8, 1) * F + f
    first = np.full(N * 8 * F, P); np.minimum.at(first, key[m], lane[m])
    return m & (first[key] == lane)
def reference(sf, pw, ot, x0, dr, c0, th, hw):
    cells = sf.astype(np.int64).reshape(N, 8, 16, C); w = pw.astype(np.float32).astype(np.int32).reshape(N, 8, 16, F); o = ot.astype(np.int64).reshape(N, 8, L, F)
    x = x0.astype(np.float32).astype(np.int32).reshape(N, 8, 16, P); step = dr.astype(np.float32).astype(np.int32).reshape(N, 8, 16, P); hv = hw.astype(np.float32).astype(np.int64).reshape(N, 8, 16, 2)
    c = np.stack([gentries(a) for a in c0]).astype(np.int64); t = np.stack([gentries(a) for a in th]).astype(np.int64)
    d = c.copy(); j = np.full((N, 8, P), -1); f = np.zeros((N, 8, P), np.int64)
    rk = np.arange(N)[:, None, None]; gr = np.arange(8)[None, :, None]
    for rnd in range(RO):
        for sub in range(T):
            live = j < L
            code = np.take_along_axis(cells, d[:, :, None, :], 3); su = code >> 1
            v = np.stack([np.add.reduce(np.take_along_axis(w, su[:, :, i:i + 1], 3) * x, axis=2) for i in range(16)], axis=2)
            v = np.where((code & 1) == 1, -v, v)
            inside = live & (np.add.reduce((v >= 0).astype(np.int64), axis=2) >= t); miss = live & ~inside
            a, b, p = np.nonzero(lowest(inside & (j > 0), f)); ff, jj = f[a, b, p], j[a, b, p]
            up, lo = o[a, b, jj - 1, ff], o[a, b, jj, ff]
            o[a, b, jj - 1, ff] = lo; o[a, b, jj, ff] = up
            c = np.where(inside, d, c); x = np.where(inside[:, :, None, :], (x + step) & 15, x)
            least = np.take_along_axis(su, np.argmin(v, axis=2)[:, :, None, :], 2)[:, :, 0]
            f = np.where(miss & (j == -1), least, f)
            j = np.where(inside, -1, np.where(miss, j + 1, j))
            d = np.where(miss & (j < L), o[rk, gr, np.clip(j, 0, L - 1), f], d)
        wait = j == L; q = f % N; served = np.zeros((N, 8, P), bool)
        for k in range(N):
            m = wait & (q == k); n = m.astype(np.int64)
            served = served | (m & (np.add.accumulate(n, axis=2) - n < CAP))
        wq = hv[q, gr]; xt = x.transpose(0, 1, 3, 2).astype(np.int64)
        h = ((np.add.reduce(xt * wq[..., 0], axis=3) * np.add.reduce(xt * wq[..., 1], axis=3)) >> 5) & (F - 1)
        ans = o[q, gr, 0, h]
        a, b, p = np.nonzero(lowest(served, f)); o[a, b, L - 1, f[a, b, p]] = ans[a, b, p]
        d = np.where(served, ans, d); j = np.where(served, L - 1, j)
    return {"yt": o.reshape(N, 8 * L, F).astype(np.float32), "yc": np.stack([gtable(a) for a in c]).astype(np.float32), "yx": x.reshape(N, 128, P).astype(np.float32)}

@@ -1,0 +1,646 @@
+from concourse.bass import DstId, RemoteDMATransfer
+from concourse.mybir import AluOpType as A, ActivationFunctionType as AF
+
+NR, NSUB, NROUND = 4, 4, 3
+FF = 4096
+LW = FF + 256
+SPLIT = {"plain": (64, 20), "epoch": (128, 12), "req": (48, 8), "first": (64, 16), "second": (80, 16), "afterx": (80, 8)}
+EARLY = 2
+
+F32, B16, I32, U16 = "float32", "bfloat16", "int32", "uint16"
+SCRATCH = {}
+for _t, _bufs in (
+        (F32, dict(sff=[2048], LL=[LW], otf=[1024], cf=[256], ww=[8, 32], wc=[128], mx=[256], th1=[16], tha=[16], thb=[16],
+                   th3=[16, 3], thp=[16, 3], p2=[16, 2],
+                   p4=[16, 4], a2=[16, 2], cc=[16], ff=[16], fk=[16], df=[16], zz=[16], t1=[16], t2=[16], xso=[128],
+                   xro=[128], xrk=[128], xdd=[128], xhh=[128], r3=[256], nn=[256], nt=[16, 16], nt2=[16, 16], idf=[128],
+                   nid=[128], idm=[128], onf=[128], z16=[32], gm=[8], col=[16], kmin=[128], selr=[8, 3], seld=[8, 2],
+                   coef=[2], dmt=[16], dml=[16], hr=[16], oh=[64], ua=[64], ub=[64], osv=[64], dk=[16], rp0=[64], rp1=[64],
+                   rp2=[64], ro0=[48], ro1=[48], ro2=[48], rg=[1024], xf=[256], ycf=[16])),
+        (B16, dict(pwn=[FF], pw2=[2 * FF], xx0=[512], xx1=[512], drs=[256], xb=[2048], gg=[4096], sg=[256], hwa=[4, 8],
+                   hwb=[4, 8, 2], ge=[128], cn=[256], nu=[128], fl0=[16, 5], fl1=[16, 5], xxo=[128], fat=[16, 16],
+                   fbt=[16, 16], fan=[256], fao=[256], fbn=[256], eq=[8, 384], idb=[128], id8=[128], trb=[128], trp=[128],
+                   onb=[128], zb=[64], z16b=[32], k01=[128], plb=[16], c256=[16], wh=[64], srv=[16])),
+        (I32, dict(sfw=[2048], oti=[1024], c0i=[16], thi=[16], fi=[16], fj=[16], dig=[16, 3], ia=[16], ib=[16], ic=[16])),
+        (U16, dict(cu=[256], uso=[16], uro=[16], uxo=[16], udd=[16], xl=[2], rq0=[64], rq1=[64], rq2=[64]))):
+    for _k in _bufs:
+        SCRATCH[_k] = ("sbuf", [128] + _bufs[_k], _t)
+for _i in range(8):
+    SCRATCH["b%d" % _i] = ("psum", [128, 512], F32)
+SEMAPHORES = ["qV", "qS", "qP", "qG", "sent", "hwin"] + ["d%d" % i for i in range(32)] + \
+    ["rqin%d" % i for i in range(3)] + ["rpin%d" % i for i in range(3)]
+
+
+def emit(g, T, ops):
+    Q = {"V": g.vector, "S": g.scalar, "P": g.tensor, "G": g, "Y": g.sync}
+    lastw, readers, bank = {}, {}, {}
+    seen = {q: {} for q in Q}
+    for i, o in enumerate(ops):
+        q = o["q"]
+        deps = set((lastw[k], True) for k in o["r"] if k in lastw)
+        for k in o["w"]:
+            if k in lastw:
+                deps.add((lastw[k], False))
+            deps.update((j, False) for j in readers.get(k, []))
+        for k in o["b"]:
+            deps.update((j, False) for j in bank.setdefault(k, {}).values())
+            bank[k][q] = i
+        need = {}
+        for j, raw in deps:
+            p = ops[j]
+            if p["tok"] is not None:
+                need[("tok", j)] = j
+            elif p["q"] != q or raw:
+                need[p["q"]] = max(need.get(p["q"], -1), j)
+        o["waits"] = []
+        for k in sorted(need, key=str):
+            j = need[k]
+            if seen[q].get(k, -1) < j:
+                seen[q][k] = j
+                o["waits"].append(j)
+                ops[j]["inc"] = True
+        for k in o["r"]:
+            readers.setdefault(k, []).append(i)
+        for k in o["w"]:
+            lastw[k] = i
+            readers[k] = []
+    cnt = {q: 0 for q in Q}
+    last = {}
+    for o in ops:
+        if o["tok"] is not None:
+            o["val"] = last[o["tname"]] = o["tok"]
+        elif o["inc"]:
+            cnt[o["q"]] += 1
+            o["val"] = (T.sem["q" + o["q"]], cnt[o["q"]])
+    for o in ops:
+        e = Q[o["q"]]
+        for j in o["waits"]:
+            e.wait_ge(*ops[j]["val"])
+        if o["fn"] is None:
+            continue
+        ins = o["fn"](e)
+        if o["dma"]:
+            ins.then_inc(o["tok"][0], 16)
+        elif o["tok"] is None and o["inc"]:
+            ins.then_inc(o["val"][0], 1)
+    for k in last:
+        g.sync.wait_ge(*last[k])
+
+
+def rank_program(g, core, T, topo):
+    me = T.rank_of(core)
+    if me is None:
+        return
+    ops = []
+    nd = [0]
+    sent = [0]
+
+    def op(q, fn, r=(), w=(), b=(), tname=None, val=0, isdma=False):
+        ops.append(dict(q=q, fn=fn, r=list(r), w=list(w), b=list(b), tok=(T.sem[tname], val) if tname else None,
+                        tname=tname, inc=False, dma=isdma))
+
+    def dma(q, out, in_, r=(), w=()):
+        nd[0] += 1
+        op(q, lambda e: e.dma_start(out, in_), r, w, (), "d%d" % (nd[0] - 1), 16, True)
+
+    def arrive(name, val, w):
+        op("G", None, (), w, (), name, val)
+
+    def remote(trs, n, r):
+        sent[0] += n
+        op("G", lambda e: e.remote_dma_fused(trs, local_sem=T.sem.sent), r, (), (), "sent", sent[0])
+
+    def cp(out, in_, r, w, b=()):
+        op("V", lambda e: e.tensor_copy(out, in_), r, w, b)
+
+    def tt(out, a, c, o, r, w, b=()):
+        op("V", lambda e: e.tensor_tensor(out, a, c, o), r, w, b)
+
+    def ts(out, a, s1, o0, r, w, s2=None, o1=None, b=()):
+        if o1 is None:
+            op("V", lambda e: e.tensor_scalar(out, a, s1, None, o0), r, w, b)
+        else:
+            op("V", lambda e: e.tensor_scalar(out, a, s1, s2, o0, o1), r, w, b)
+
+    def scan(out, d0, d1, o0, o1, r, w, b=()):
+        op("V", lambda e: e.tensor_tensor_scan(out, d0, d1, 0.0, o0, o1), r, w, b)
+
+    def ms(ap, v, w, b=()):
+        op("V", lambda e: e.memset(ap, v), w, w, b)
+
+    def act(out, in_, f, r, w, b=(), **kw):
+        op("S", lambda e: e.activation(out, in_, f, **kw), r, w, b)
+
+    def mm(out, l, rr, st, sp, r, b):
+        op("P", lambda e: e.matmul(out, l, rr, st, sp), r, (), b)
+
+    peers = [(me + s) % NR for s in range(1, NR)]
+    dst = {}
+    for r in peers:
+        rid, pid, _ = topo.addr(T.cores[r])
+        dst[r] = DstId(rid=rid, pnc=pid)
+    eng = [e for e in topo.engines(core, T.cores[peers[0]]) if all(e in topo.engines(core, T.cores[r]) for r in peers)]
+    ne = len(eng)
+    bits = lambda es: sum(1 << e for e in es)
+    share = [eng[:ne // 2], eng[ne // 2:3 * ne // 4], eng[3 * ne // 4:]]
+    B = {k: T["b%d" % i] for i, k in enumerate(["V0", "V1", "CT", "NB", "EA", "EB", "S1", "S2"])}
+    XL = T.xl[:, 0:1]
+
+    def conv(bk, c0, xs, base=None):
+        lo = xs[0] == "xxo"
+        z = T.z16b if lo else T.z16
+        if base:
+            mm(B[bk][:, c0:c0 + 16], (T.idb if lo else T.idf)[:], T[base][:], True, False, [base], [bk])
+        for qd in range(4):
+            for n, x in enumerate(xs):
+                mm(B[bk][32 * qd:32 * qd + 32, c0:c0 + 16], z[:, 0:32], T[x][:, 32 * qd + 16:32 * qd + 32],
+                   not base and n == 0, False, [x], [bk])
+                mm(B[bk][32 * qd:32 * qd + 16, c0:c0 + 16], z[:, 16:32], T[x][:, 32 * qd:32 * qd + 16], False,
+                   n == len(xs) - 1, [x], [bk])
+
+    dma("Y", T.c0i[:], T.c0[:], w=["c0i"])
+    dma("S", T.xx0[:, 0:256], T.x0[:], w=["xc0"])
+    dma("Y", T.thi[:], T.th[:], w=["thi"])
+    dma("S", T.hwa[:, me, 0:2], T.hw[:], w=["hwo"])
+    dma("Y", T.sfw[:], T.sf[:], w=["sf"])
+    for k in range(4):
+        dma("Y", T.pwn[:, 1024 * k:1024 * k + 1024], T.pw[:, 1024 * k:1024 * k + 1024], w=["pw%d" % k])
+    dma("Y", T.drs[:], T.dr[:], w=["dr"])
+    for k in range(3):
+        dma("Y", T.oti[32 * k:32 * k + 32, :], T.ot[k::3, :], w=["oti%d" % k])
+
+    ms(T.onf[:], 1.0, ["onf"])
+    ms(T.onb[:], 1.0, ["onb"])
+    op("G", lambda e: e.iota(T.ia[:], [[-1, 16]], 0, 1), (), ["ia"])
+    op("G", lambda e: e.iota(T.ib[:, 0:8], [[-16, 8]], 0, 1), (), ["ib"])
+    op("G", lambda e: e.iota(T.ic[:], [[16, 16]], 0, 1), (), ["ic"])
+    op("G", lambda e: e.affine_select(T.idf[:], T.onf[:], [[-1, 128]], A.is_equal, 0.0, 0, 1), ["onf"], ["idf"])
+    op("G", lambda e: e.iota(T.dmt[:], [[128, 2], [0, 8]], FF, 1, allow_small_or_imprecise_dtypes=True), (), ["dmt"])
+    op("G", lambda e: e.affine_select(T.trp[:], T.onb[:], [[1, 128]], A.is_gt, 0.0, 0, -1), ["onb"], ["trp"])
+    op("G", lambda e: e.iota(T.LL[:], [[0, LW]], 0, 0, allow_small_or_imprecise_dtypes=True), (), ["LLz"])
+    remote([RemoteDMATransfer(dst_ids=[dst[r] for r in peers], dma_engine_mask=bits(eng), remote_sem=T.sem.hwin,
+                              srcs=[T.hwa[:, me, 0:2]], dsts=[T.hwa[:, me, 0:2] for r in peers])], ne, ["hwo"])
+    arrive("hwin", 3 * ne, ["hwr"])
+    for n, x in enumerate((T.xso, T.xro, T.xrk, T.xdd, T.xhh, T.xxo)):
+        ms(x[:], 0.0, ["x0s%d" % n])
+    ms(T.z16[:, 0:16], 0.0, ["z0"])
+    ts(T.fi[:], T.ia[:], 15, A.bitwise_and, ["ia"], ["fi"])
+    ts(T.fj[:, 0:8], T.ib[:, 0:8], 4, A.arith_shift_right, ["ib"], ["fj"])
+    pc = T.ic[:, 0:1]
+    ts(T.dig[:, 0, 0:1], pc, 7, A.bitwise_and, ["ic"], ["dg0"])
+    ts(T.dig[:, 0, 1:2], pc, 8, A.bitwise_and, ["ic"], ["dg1"])
+    ts(T.dig[:, 0, 2:3], pc, 4, A.arith_shift_right, ["ic"], ["dg2"])
+    ts(T.dig[:, 1, 0:1], pc, 15, A.bitwise_and, ["ic"], ["dg3"])
+    ts(T.dig[:, 1, 1:2], pc, 4, A.arith_shift_right, ["ic"], ["dg4"], 1, A.bitwise_and)
+    ts(T.gm[:], T.fj[:, 0:8], 0.0, A.is_equal, ["fj"], ["gm"])
+    ts(T.z16[:, 16:32], T.fi[:], 0.0, A.is_equal, ["fi"], ["z1"])
+    cp(T.col[:, 0:3], T.dig[:, 0, 0:3], ["dg0", "dg1", "dg2"], ["colA"])
+    cp(T.col[:, 3:5], T.dig[:, 1, 0:2], ["dg3", "dg4"], ["colB"])
+    ms(B["V0"][:, 0:256], 0.0, [], ["V0"])
+    ts(T.t1[:, 0:1], T.col[:, 0:1], 16.0, A.mult, ["colA"], ["t1"], T.col[:, 1:2], A.add)
+    ts(T.t2[:, 0:1], T.col[:, 2:3], -16.0, A.mult, ["colA"], ["t2"])
+    ts(T.col[:, 5:6], T.col[:, 3:4], -8192.0, A.mult, ["colB"], ["colC"], 8192.0 * 15, A.add)
+    cp(T.z16b[:], T.z16[:], ["z0", "z1"], ["z16b"])
+    cp(T.idb[:], T.idf[:], ["idf"], ["idb"])
+    ts(T.xl[:, 0:1], T.t1[:, 0:1], T.col[:, 2:3], A.add, ["t1", "colA"], ["xl"])
+    ts(T.plb[:], T.ic[:], T.t2[:, 0:1], A.add, ["t2", "ic"], ["plb"])
+    op("P", None, ["z0", "z1", "z16b", "idb", "idf"])
+    ms(B["V1"][:, 0:256], 0.0, [], ["V1"])
+    cp(T.udd[:], T.c0i[:], ["c0i"], ["udd"])
+    op("V", None, ["xl", "x0s5"])
+    cp(T.xdd[:].indirect(XL), T.c0i[:], ["c0i"], ["xdd"])
+    conv("S2", 0, ["xdd"])
+    cp(T.xro[:].indirect(XL), T.thi[:], ["thi"], ["xro"])
+    conv("S1", 0, ["xro"])
+
+    def spread_x(x, xk):
+        for g8 in range(8):
+            act(T.xb[:, 256 * g8:256 * g8 + 256], x[:, 0:256], AF.Copy, [xk, "gm"], ["xb%d" % g8], scale=T.gm[:, g8:g8 + 1])
+
+    spread_x(T.xx0, "xc0")
+    ms(T.kmin[:], -0.0625, ["kmin"])
+    ms(T.k01[:], 1.0, ["k01"])
+    ms(T.fl1[:], 0.0, ["fl1"])
+    ms(T.fat[:], 0.0, ["fat"])
+    ms(T.fbt[:], 0.0, ["fbt"])
+    ms(T.nt[:], 0.0, ["nt"])
+    ms(T.kmin[:, 0::16], 8192.0, ["kmin"])
+    ms(T.k01[:, 0::16], 0.0, ["k01"])
+    ms(T.fl1[:, :, 4], 1.0, ["fl1"])
+    ms(T.fat[:, :, 6:9], -0.5, ["fat"])
+    ms(T.fbt[:, :, 3:6], -0.5, ["fbt"])
+    ms(T.fk[:], 0.0, ["fk"])
+    ms(T.c256[:], 256.0, ["c256"])
+    ms(T.zb[:], 0.0, ["zb"])
+    ms(T.col[:, 7:8], -15.5, ["colE"])
+    ms(T.col[:, 8:9], -8.0, ["colF"])
+    cp(T.p4[:, :, 3], B["S2"][:, 0:16], [], ["dd"], ["S2"])
+    cp(T.cc[:], B["S2"][:, 0:16], [], ["cc"], ["S2"])
+    for s in range(3):
+        ts(T.th3[:, :, s], B["S1"][:, 0:16], 1.0 / 32, A.mult, [], ["th3"], b=["S1"])
+    ts(T.thb[:], B["S1"][:, 0:16], 1.0 / 32, A.mult, [], ["thb"], b=["S1"])
+    ts(T.th1[:], B["S1"][:, 0:16], 1.0 / 32, A.mult, [], ["th1"], 1.0, A.add, b=["S1"])
+    act(T.nid[:], T.idf[:], AF.Copy, ["idf"], ["nid"], scale=-1.0)
+    act(T.id8[:], T.idb[:], AF.Copy, ["idb"], ["id8"], scale=-8.0)
+    tt(T.coef[:, 0:1], T.z16[:, 17:18], T.z16[:, 16:17], A.subtract, ["z1"], ["cf0"])
+    tt(T.coef[:, 1:2], T.z16[:, 17:18], T.z16[:, 18:19], A.subtract, ["z1"], ["cf1"])
+    ts(T.col[:, 6:7], T.z16[:, 16:17], -1.0, A.mult, ["z1"], ["colD"], 1.0, A.add)
+    tt(T.thp[:], T.fl1[:, :, 2:5], T.th3[:], A.mult, ["fl1", "th3"], ["thp"])
+    ts(T.dml[:], T.plb[:], float(FF), A.add, ["plb"], ["dml"])
+    ts(T.trb[:], T.trp[:], 64.0, A.mult, ["trp"], ["trb"], -64.0, A.add)
+    for g8 in range(8):
+        act(T.selr[:, g8, :], T.z16[:, 16:19], AF.Copy, ["z1", "gm"], ["selr"], scale=T.gm[:, g8:g8 + 1])
+        act(T.seld[:, g8, :], T.coef[:], AF.Copy, ["cf0", "cf1"], ["seld"], scale=T.gm[:, g8:g8 + 1])
+    act(T.idm[:], T.idf[:], AF.Copy, ["idf", "colD"], ["idm"], scale=T.col[:, 6:7])
+    ms(T.nt2[:], 0.0, ["nt2"])
+    cp(T.cu[:], T.sfw[:].indirect(T.udd[:]), ["sf", "udd"], ["cu"])
+    cp(T.sff[:], T.sfw[:], ["sf"], ["sff"])
+    PW = []
+    for k in range(4):
+        c, m = 1024 * k, 1024 * k + (768 if k < 3 else 512)
+        ts(T.pw2[:, 2 * c + 1:2 * c + 2048:2], T.pwn[:, c:c + 1024], -1.0, A.mult, ["pw%d" % k], ["pa%d" % k])
+        act(T.pw2[:, 2 * c:2 * m:2], T.pwn[:, c:m], AF.Copy, ["pw%d" % k], ["pb%d" % k])
+        cp(T.pw2[:, 2 * m:2 * c + 2048:2], T.pwn[:, m:c + 1024], ["pw%d" % k], ["pc%d" % k])
+        PW += ["pa%d" % k, "pb%d" % k, "pc%d" % k]
+    LLK = ["LL0", "LL1", "LL2"]
+
+    def blockers(av, ak, part):
+        nb = B["S1"]
+        if part != 1:
+            mm(nb[:, 0:16], T.idb[:], T.zb[:, 0:16], True, False, ["zb"], ["S1"])
+            mm(nb[:, 0:8], T.id8[:], av(0, 8), False, False, ["id8", ak[0]], ["S1"])
+            for g8 in range(8):
+                mm(nb[:, g8:g8 + 1], T.eq[:, g8, 0:128], av(g8, g8 + 1), False, False, ["eq%d" % g8], ["S1"])
+                mm(nb[:, 8 + g8:9 + g8], T.eq[:, g8, 128:256], av(g8, g8 + 1), False, False, ["eq%d" % g8, ak[0]], ["S1"])
+        if part != 0:
+            mm(nb[:, 8:16], T.id8[:], av(8, 16), False, False, [ak[1]], ["S1"])
+            for g8 in range(8):
+                mm(nb[:, 8 + g8:9 + g8], T.eq[:, g8, 256:384], av(8 + g8, 9 + g8), False, g8 == 7, ["eq%d" % g8, ak[1]], ["S1"])
+
+    def write_offsets():
+        ts(T.zz[:], B["S1"][:, 0:16], -8.0, A.is_equal, [], ["zz"], b=["S1"])
+        tt(T.xso[:].indirect(XL), T.zz[:], T.df[:], A.mult, ["zz", "df"], ["xso"])
+        conv("S2", 0, ["xso"], "dml")
+
+    def values_old(idm):
+        mm(B["NB"][:, 0:256], T[idm][:], T.r3[:], True, False, ["r3", idm], ["NB"])
+
+    def values_new(nt):
+        for h in range(2):
+            mm(B["NB"][:, 128 * h:128 * h + 128], T[nt][:, 8 * h:8 * h + 8, :], T.idf[:], False, h == 1, [nt], ["NB"])
+
+    def epoch_v():
+        cp(T.fi[:], T.ff[:], ["ff"], ["fi"])
+        ts(T.dig[:, :, 0], T.fi[:], 15, A.bitwise_and, ["fi"], ["dg0"])
+        ts(T.dig[:, :, 1], T.fi[:], 4, A.arith_shift_right, ["fi"], ["dg1"], 15, A.bitwise_and)
+        ts(T.dig[:, :, 2], T.fi[:], 8, A.arith_shift_right, ["fi"], ["dg2"])
+        cp(T.fat[:, :, 0:3], T.dig[:], ["dg0", "dg1", "dg2", "fat"], ["fa0"])
+
+    def epoch_features():
+        act(T.fbt[:, :, 0:3], T.fat[:, :, 0:3], AF.Copy, ["fa0", "fbt"], ["fb0"])
+        act(T.fat[:, :, 3:6], T.fat[:, :, 0:3], AF.Square, ["fa0"], ["fa1"])
+        act(T.fbt[:, :, 6:9], T.fat[:, :, 0:3], AF.Square, ["fa0"], ["fb1"])
+        for h in range(2):
+            mm(B["EA"][:, 128 * h:128 * h + 128], T.fat[:, 8 * h:8 * h + 8, :], T.idb[:], True, True, ["fa0", "fa1"], ["EA"])
+        for h in range(2):
+            mm(B["EB"][:, 128 * h:128 * h + 128], T.fbt[:, 8 * h:8 * h + 8, :], T.idb[:], True, True, ["fb0", "fb1"], ["EB"])
+        act(T.fan[:], B["EA"][:, 0:256], AF.Copy, [], ["fan"], ["EA"])
+        act(T.fbn[:], B["EB"][:, 0:256], AF.Copy, [], ["fbn"], ["EB"])
+        act(T.fao[:], B["EA"][:, 0:256], AF.Copy, ["colB"], ["fao"], ["EA"], scale=T.col[:, 4:5])
+
+    def epoch_pairs(n0, n1):
+        for n in range(n0, n1):
+            g8 = (0, 2, 4, 6, 1, 3, 5, 7)[n]
+            bk = "EB" if n % 2 == 0 else "EA"
+            p0 = 32 * (g8 // 2)
+            p1 = p0 + (32 if g8 % 2 else 16)
+            fa = "fao" if g8 % 2 else "fan"
+            mm(B[bk][:, 0:256], T[fa][p0:p1, 0:128], T.fbn[p0:p1, 0:256], True, False, [fa, "fbn"], [bk])
+            mm(B[bk][:, 0:128], T.idb[:], T.trb[:], False, True, ["trb"], [bk])
+            mm(B[bk][:, 256:384], T[fa][p0:p1, 128:256], T.fbn[p0:p1, 128:256], True, False, [fa, "fbn"], [bk])
+            mm(B[bk][:, 256:384], T.idb[:], T.trb[:], False, True, [], [bk])
+            act(T.eq[:, g8, :], B[bk][:, 0:384], AF.Relu, ["onf"], ["eq%d" % g8], [bk], bias=T.onf[:, 0:1], scale=2.0)
+
+    def request_sums(xc, xk):
+        for r in range(NR):
+            for h in range(2):
+                c0 = 128 + 32 * r + 16 * h
+                mm(B["S1"][:, c0:c0 + 16], xc[:, 128 * h:128 * h + 128], T.hwb[:, r, :, :], True, True, [xk, "hwb"], ["S1"])
+
+    def request():
+        cp(T.fi[:], T.ff[:], ["ff"], ["fi"])
+        ts(T.fj[:], T.fi[:], 3, A.bitwise_and, ["fi"], ["fj"])
+        for r in range(NR):
+            ts(T.oh[:, 16 * r:16 * r + 16], T.fj[:], float(r), A.is_equal, ["fj"], ["oh"])
+        cp(T.hr[:], T.fj[:], ["fj"], ["hr"])
+        tt(T.ua[:], B["S1"][:, 128:256:2], T.oh[:], A.mult, ["oh"], ["ua"], ["S1"])
+        tt(T.ub[:], B["S1"][:, 129:256:2], T.ua[:], A.mult, ["ua"], ["ub"], ["S1"])
+        tt(T.ua[:, 0:32], T.ub[:, 0:32], T.ub[:, 32:64], A.add, ["ub"], ["ua"])
+        tt(T.fi[:], T.ua[:, 0:16], T.ua[:, 16:32], A.add, ["ua"], ["fi"])
+        ts(T.fj[:], T.fi[:], 5, A.arith_shift_right, ["fi"], ["fj"], FF - 1, A.bitwise_and)
+        cp(T.xhh[:].indirect(XL), T.fj[:], ["fj"], ["xhh"])
+
+    def request_send(rnd):
+        rq = T["rq%d" % rnd]
+        cp(rq[:, 0:16], B["S2"][:, 16:32], [], ["rqo%d" % rnd], ["S2"])
+        remote([RemoteDMATransfer(dst_ids=[dst[r] for r in peers], dma_engine_mask=bits(eng), remote_sem=T.sem["rqin%d" % rnd],
+                                  srcs=[rq[:, 0:16]], dsts=[rq[:, 16 * s:16 * s + 16] for s in range(1, NR)])], ne, ["rqo%d" % rnd])
+        arrive("rqin%d" % rnd, 3 * ne, ["rqi%d" % rnd])
+
+    def answer(rnd):
+        rq, ro, rp = T["rq%d" % rnd], T["ro%d" % rnd], T["rp%d" % rnd]
+        win = T.LL[:, 0:FF]
+        for c in (2, 3, 4):
+            cp(T.rg[:, 128 * c:128 * c + 128], win.indirect(rq[:, 8 * c:8 * c + 8]), LLK + ["rqi%d" % rnd], ["rg%d" % c])
+            act(T.rg[:, 128 * c + 384:128 * c + 512], win.indirect(rq[:, 8 * c + 24:8 * c + 32]), AF.Copy,
+                LLK + ["rqi%d" % rnd], ["rg%d" % (c + 3)])
+        for c in (2, 5, 3, 6, 4, 7):
+            mm(B["EA"][:, 8 * c:8 * c + 8], T.rg[:, 128 * c:128 * c + 128], T.selr[:, :, 2], True, True, ["rg%d" % c, "selr"], ["EA"])
+        act(ro[:], B["EA"][:, 16:64], AF.Copy, [], ["ro%d" % rnd], ["EA"])
+        remote([RemoteDMATransfer(dst_ids=[dst[(me - s) % NR]], dma_engine_mask=bits(share[s - 1]), remote_sem=T.sem["rpin%d" % rnd],
+                                  src=ro[:, 16 * s - 16:16 * s], dst=rp[:, 16 * me:16 * me + 16]) for s in range(1, NR)],
+               ne, ["ro%d" % rnd])
+        arrive("rpin%d" % rnd, ne, ["rpi%d" % rnd])
+        act(T.rg[:, 0:256], win.indirect(rq[:, 0:16]), AF.Copy, LLK + ["rqo%d" % rnd], ["rg0"])
+
+    def answer_own(rnd):
+        for c in range(2):
+            mm(B["EB"][:, 8 * c:8 * c + 8], T.rg[:, 128 * c:128 * c + 128], T.selr[:, :, 2], True, True, ["rg0"], ["EB"])
+        act(T["rp%d" % rnd][:, 16 * me:16 * me + 16], B["EB"][:, 0:16], AF.Copy, [], ["rpo%d" % rnd], ["EB"])
+
+    def planes(q, a, b):
+        if a < b:
+            src, w = T.pw2[:].indirect(T.cu[:, a:b]), ["G%d" % p for p in range(a, b)]
+            if q == "V":
+                cp(T.gg[:, 16 * a:16 * b], src, PW + ["cu"], w)
+            else:
+                act(T.gg[:, 16 * a:16 * b], src, AF.Copy, PW + ["cu"], w)
+
+    XB = ["xb%d" % i for i in range(8)]
+
+    def dots(a, b):
+        for p in range(a, b):
+            h, qd, n = p // 128, (p % 128) // 32, p % 32
+            mm(B["V%d" % h][32 * qd:32 * qd + 16, n:256:32], T.gg[:, 16 * p:16 * p + 16], T.xb[:, p::256], True, True,
+               ["G%d" % p] + XB, ["V%d" % h])
+
+    WW = T.ww[:, :, 0:16]
+    MS = B["CT"][:, 256:384]
+    CNT = T.cn[:, 15::16]
+
+    def test(h, fl, fk, swaps):
+        op("V", lambda e: e.transpose(T.ww[:], B["V%d" % h][:, 0:256]), [], ["ww"], ["V%d" % h])
+        ts(T.ge[:], WW, 0.0, A.is_ge, ["ww"], ["ge"], 1.0 / 32, A.mult)
+        if h:
+            act(T.wc[:], WW, AF.Copy, ["ww"], ["wc"])
+        else:
+            cp(T.wc[:], WW, ["ww"], ["wc"])
+        scan(T.cn[:, 128 * h:128 * h + 128], T.k01[:], T.ge[:], A.mult, A.add, ["ge", "k01"], ["cn%d" % h])
+        c, cnt = slice(8 * h, 8 * h + 8), T.cn[:, 128 * h + 15:128 * h + 128:16]
+        if not h:
+            least_a()
+        if swaps:
+            tt(fl[:, c, 0], cnt, T.tha[:, c], A.is_ge, ["cn%d" % h, "tha"], [fk + "a%d" % h])
+        tt(fl[:, c, 4], cnt, T.thb[:, c], A.is_ge, ["cn%d" % h, "thb"], [fk + "b%d" % h])
+
+    def least_a():
+        scan(MS, T.kmin[:], T.wc[:], A.add, A.min, ["wc", "kmin"], ["ms"], ["CT"])
+
+    def least_b():
+        tt(T.nu[:], MS, T.wc[:], A.not_equal, ["ms", "wc"], ["nu"], ["CT"])
+
+    def least_c(h):
+        scan(T.mx[:, 128 * h:128 * h + 128], T.nu[:], B["CT"][:, 128 * h:128 * h + 128], A.mult, A.max, ["nu"], ["mx%d" % h], ["CT"])
+
+    pending = []
+    NT = NSUB * NROUND
+    for t in range(NT):
+        rnd, last_sub, end = t // NSUB, t % NSUB == NSUB - 1, t == NT - 1
+        fk, fok = "fl%d" % (t % 2), "fl%d" % (1 - t % 2)
+        fl, fo = T[fk], T[fok]
+        FK, FOK = [[k, k + "b0", k + "b1"] for k in (fk, fok)]
+        xc, xn = T["xx%d" % (t % 2)], T["xx%d" % (1 - t % 2)]
+        xck, xnk, xk1 = "xc%d" % (t % 2), "xc%d" % (1 - t % 2), "xn%d" % (t % 2)
+        swaps = t >= 2
+        epoch = swaps and t % 2 == 0
+        kind = ("first", "second")[t] if t < 2 else "req" if last_sub else "plain" if not epoch else "epoch" if t % NSUB else "afterx"
+        a0, a1 = SPLIT[kind]
+        a1 += 128
+        if t:
+            cp(T.cu[:], T.sfw[:].indirect(T.udd[:]), ["sf", "udd"], ["cu"])
+        act(T.cf[:], T.sff[:].indirect(T.udd[:]), AF.Identity, ["sff", "udd", "colC"], ["cf"], bias=T.col[:, 5:6])
+        if kind == "afterx":
+            act(T.nn[:], B["NB"][:, 0:256], AF.Copy, [], ["nn"], ["NB"])
+            write_offsets()
+        if last_sub:
+            request_sums(xc, xck)
+        if epoch:
+            epoch_pairs(EARLY if kind == "afterx" else 0, 8)
+        planes("S", a0, 128)
+        m1 = (a1 + 256) // 4 * 2
+        m2 = (m1 + 256) // 4 * 2
+        planes("S", a1, m1)
+        planes("S", m1, m2)
+        planes("S", m2, 256)
+        planes("V", 0, a0 // 2)
+        for h in range(2):
+            op("P", lambda e, h=h: e.transpose(B["CT"][:, 128 * h:128 * h + 128], T.cf[:, 128 * h:128 * h + 128], T.idf[:]),
+               ["cf"], [], ["CT"])
+        mm(B["EB"][:, 0:256], T.idb[:], xc[:, 0:256], True, False, [xck], ["EB"])
+        mm(B["EB"][:, 0:256], T.idb[:], T.drs[:], False, True, ["dr"], ["EB"])
+        dots(0, a0 // 2)
+        if t == 0:
+            cp(T.otf[0:96, :], T.oti[0:96, :], ["oti0", "oti1", "oti2"], ["otf"])
+            for k in range(3):
+                dma("Y", T.LL[2 - k::16, 0:FF], T.otf[32 * k:32 * k + 32, :], r=["otf", "LLz"], w=["LL%d" % k])
+        if t == 1:
+            for g8 in range(8):
+                ts(T.hwb[:, :, g8, :], T.hwa[:, :, 0:2], T.gm[:, g8:g8 + 1], A.mult, ["hwo", "hwr", "gm"], ["hwb"])
+        for fn in pending:
+            fn()
+        del pending[:]
+        if last_sub:
+            request()
+        dots(a0, 128)
+        if last_sub:
+            conv("S2", 16, ["xhh"])
+        planes("V", a0 // 2, a0)
+        if last_sub:
+            request_send(rnd)
+        planes("V", 128, a1)
+        dots(a0 // 2, a0)
+        if swaps:
+            values_old("idf")
+            values_new("nt")
+        dots(128, 256)
+        test(0, fl, fk, swaps)
+        least_b()
+        least_c(0)
+        av = lambda a, b, fl=fl: fl[:, a:b, 0]
+        if swaps:
+            blockers(av, [fk + "a0", fk + "a1"], 0)
+        act(T.sg[:], B["EB"][:, 0:256], AF.Sign, ["colE"], ["sg"], ["EB"], bias=T.col[:, 7:8])
+        mm(B["EA"][:, 0:256], T.idb[:], xc[:, 0:256], True, False, [xck], ["EA"])
+        mm(B["EA"][:, 0:256], T.idb[:], T.drs[:], False, False, [], ["EA"])
+        mm(B["EA"][:, 0:256], T.id8[:], T.sg[:], False, True, ["sg", "id8"], ["EA"])
+        test(1, fl, fk, swaps)
+        if swaps:
+            act(T.nn[:], B["NB"][:, 0:256], AF.Copy, [], ["nn"], ["NB"])
+            blockers(av, [fk + "a0", fk + "a1"], 1)
+        act(xc[:, 256:512], B["EA"][:, 0:256], AF.Identity, ["colF"], [xk1], ["EA"], bias=T.col[:, 8:9])
+        least_a()
+        tt(T.xxo[:].indirect(XL), fl[:, :, 4], T.c256[:], A.mult, FK[1:] + ["c256"], ["xxo"])
+        conv("V1", 256, ["xxo"], "plb")
+        if swaps:
+            write_offsets()
+        least_b()
+        least_c(1)
+
+        def new_f(fo=fo, FOK=FOK):
+            tt(T.fi[:], T.mx[:, 15::16], fo[:, :, 4], A.mult, ["mx0", "mx1"] + FOK, ["fi"])
+            cp(T.uxo[:], B["V1"][:, 256:272], [], ["uxo"], ["V1"])
+            ts(T.fj[:], T.fi[:], 8191, A.bitwise_and, ["fi"], ["fj"], 1, A.arith_shift_right)
+            if swaps and not last_sub:
+                cp(T.uso[:], B["S2"][:, 0:16], [], ["uso"], ["S2"])
+            cp(T.xro[:].indirect(XL), T.fj[:], ["fj"], ["xro"])
+            conv("V0", 256, ["xrk", "xro"])
+
+        def rows(fl=fl, fk=fk):
+            for s in range(3):
+                tt(fl[:, :, 1 + s], CNT, T.thp[:, :, s], A.is_lt, ["cn0", "cn1", "thp"], [fk])
+            tt(T.ff[:], T.fj[:], T.fk[:], A.add, ["fj", "fk"], ["ff"])
+
+        if last_sub:
+            cp(T.uso[:], B["S2"][:, 0:16], [], ["uso"], ["S2"])
+        else:
+            new_f()
+        if swaps:
+            cp(T.LL[:].indirect(T.uso[:]), T.nn[:], ["nn", "uso"], LLK)
+        if last_sub:
+            answer(rnd)
+            new_f()
+            answer_own(rnd)
+        if end:
+            act(T.xf[:], xc[:].indirect(T.uxo[:]), AF.Copy, [xck, xk1, "uxo"], ["xf"])
+            for k in range(2):
+                dma("Y", T.yt[k::3, :], T.LL[2 - k::16, 0:FF], r=LLK)
+            dma("Y", T.yx[:], T.xf[:], r=["xf"])
+        else:
+            act(xn[:, 0:256], xc[:].indirect(T.uxo[:]), AF.Copy, [xck, xk1, "uxo"], [xnk])
+            if not last_sub:
+                spread_x(xn, xnk)
+            mm(B["S1"][:, 16:64], T.idb[:], T.zb[:, 0:48], True, False, ["zb"], ["S1"])
+            for s in range(3):
+                mm(B["S1"][:, 16 + s:64:3], T.nid[:], T.p4[:, :, 3], False, False, ["nid", "dd"], ["S1"])
+        if last_sub:
+            rows()
+            tt(T.p2[:], fl[:, :, 1:4:2], fl[:, :, 2:5:2], A.add, FK, ["p2"])
+            tt(T.t1[:], T.p2[:, :, 0], T.p2[:, :, 1], A.add, ["p2"], ["t1"])
+        cp(T.uro[:], B["V0"][:, 256:272], [], ["uro"], ["V0"])
+        cp(T.r3[:], T.LL[:, 0:FF].indirect(T.uro[:]), LLK + ["uro"], ["r3"])
+        if not end:
+            for h in range(2):
+                mm(B["S1"][:, 16 + 24 * h:40 + 24 * h], T.r3[:, 128 * h:128 * h + 128], T.selr[:], False, h == 1, ["r3", "selr"], ["S1"])
+        if not last_sub:
+            rows()
+        else:
+            ts(T.t2[:], T.t1[:], 8.0, A.mult, ["t1"], ["t2"])
+            tt(T.t1[:], T.t2[:], T.hr[:], A.add, ["t2", "hr"], ["t1"])
+            for r in range(NR):
+                ts(T.wh[:, 16 * r:16 * r + 16], T.t1[:], float(r), A.is_equal, ["t1"], ["wh"])
+        if not end:
+            tt(T.p4[:, :, 0:3], B["S1"][:, 16:64], fl[:, :, 1:4], A.mult, FK, ["p4"], ["S1"])
+            tt(T.a2[:], T.p4[:, :, 0:2], T.p4[:, :, 2:4], A.add, ["p4", "dd"], ["a2"])
+
+        def flags(fl=fl, FK=FK):
+            tt(T.p2[:], fl[:, :, 1:4:2], fl[:, :, 2:5:2], A.add, FK, ["p2"])
+            tt(T.t2[:], fl[:, :, 4], T.ff[:], A.mult, FK + ["ff"], ["t2"])
+            tt(T.tha[:], T.th1[:], T.p2[:, :, 0], A.subtract, ["th1", "p2"], ["tha"])
+            tt(T.thp[:], fl[:, :, 2:5], T.th3[:], A.mult, FK, ["thp"])
+            tt(T.thb[:], T.tha[:], T.p2[:, :, 1], A.subtract, ["tha", "p2"], ["thb"])
+
+        def deltas():
+            for h in range(2):
+                mm(B["S1"][:, 64 + 16 * h:80 + 16 * h], T.r3[:, 128 * h:128 * h + 128], T.seld[:], True, True, ["r3", "seld"], ["S1"])
+
+        def book(fl=fl, FK=FK, t=t):
+            tt(T.fk[:], T.ff[:], T.t2[:], A.subtract, ["ff", "t2"], ["fk"])
+            tt(T.xrk[:].indirect(XL), T.ff[:], T.t2[:], A.subtract, ["ff", "t2"], ["xrk"])
+            if t >= 1:
+                tt(T.nt[:, :, 0:3:2], B["S1"][:, 64:96], fl[:, :, 1:3], A.mult, FK, ["nt"], ["S1"])
+                tt(T.t1[:], T.nt[:, :, 0], T.nt[:, :, 2], A.add, ["nt"], ["t1"])
+                ts(T.nt[:, :, 1], T.t1[:], -1.0, A.mult, ["t1"], ["nt"])
+
+        def cells(fl=fl, FK=FK):
+            tt(T.zz[:], T.p4[:, :, 3], T.cc[:], A.subtract, ["dd", "cc"], ["zz"])
+            tt(T.df[:], T.ff[:], T.dmt[:], A.subtract, ["ff", "dmt"], ["df"])
+            tt(T.dk[:], T.zz[:], fl[:, :, 4], A.mult, ["zz"] + FK, ["dk"])
+            tt(T.cc[:], T.cc[:], T.dk[:], A.add, ["cc", "dk"], ["cc"])
+
+        if not last_sub:
+            tt(T.xdd[:].indirect(XL), T.a2[:, :, 0], T.a2[:, :, 1], A.add, ["a2"], ["xdd"])
+            conv("S2", 0, ["xdd"])
+            if t >= 1:
+                deltas()
+            tt(T.p4[:, :, 3], T.a2[:, :, 0], T.a2[:, :, 1], A.add, ["a2"], ["dd"])
+            if t % 2:
+                epoch_v()
+                epoch_features()
+                pending.append(flags)
+            else:
+                flags()
+            cp(T.udd[:], B["S2"][:, 0:16], [], ["udd"], ["S2"])
+            pending.extend([book, cells])
+            continue
+        rp = T["rp%d" % rnd]
+        mm(B["S1"][:, 128:192], T.trp[:], T.wh[:], True, False, ["wh", "trp"], ["S1"])
+        for r in range(NR):
+            mm(B["S1"][:, 136 + 16 * r:144 + 16 * r], T.onb[:], T.wh[:, 16 * r:16 * r + 8], False, r == NR - 1, ["wh", "onb"], ["S1"])
+        values_old("idm")
+        if not end:
+            tt(T.p4[:, :, 3], T.a2[:, :, 0], T.a2[:, :, 1], A.add, ["a2"], ["dd"])
+            epoch_v()
+            spread_x(xn, xnk)
+            epoch_features()
+        ts(T.ua[:], B["S1"][:, 128:192], 32.0, A.is_lt, [], ["ua"], b=["S1"])
+        tt(T.osv[:], T.ua[:], T.wh[:], A.mult, ["ua", "wh"], ["osv"])
+        tt(T.ua[:, 0:32], T.osv[:, 0:32], T.osv[:, 32:64], A.add, ["osv"], ["ua"])
+        tt(T.srv[:], T.ua[:, 0:16], T.ua[:, 16:32], A.add, ["ua"], ["srv"])
+        blockers(lambda a, b: T.srv[:, a:b], ["srv", "srv"], 2)
+        cells()
+        if end:
+            cp(T.xro[:].indirect(XL), T.cc[:], ["cc"], ["xro"])
+            write_offsets()
+            conv("V0", 256, ["xro"])
+            cp(T.uso[:], B["S2"][:, 0:16], [], ["uso"], ["S2"])
+            cp(T.ycf[:], B["V0"][:, 256:272], [], ["ycf"], ["V0"])
+            dma("Y", T.yc[:], T.ycf[:], r=["ycf"])
+        else:
+            tt(T.t1[:], T.srv[:], T.p4[:, :, 3], A.mult, ["srv", "dd"], ["t1"])
+            tt(fl[:, :, 1], fl[:, :, 1], T.srv[:], A.add, FK + ["srv"], [fk])
+            tt(T.dk[:], T.p4[:, :, 3], T.t1[:], A.subtract, ["t1", "dd"], ["dk"])
+            epoch_pairs(0, EARLY)
+            flags()
+        tt(T.ub[:], rp[:], T.osv[:], A.mult, ["rpi%d" % rnd, "rpo%d" % rnd, "osv"], ["ub"])
+        tt(T.ua[:, 0:32], T.ub[:, 0:32], T.ub[:, 32:64], A.add, ["ub"], ["ua"])
+        tt(T.nt2[:, :, 0], T.ua[:, 0:16], T.ua[:, 16:32], A.add, ["ua"], ["nt2"])
+        if not end:
+            tt(T.xdd[:].indirect(XL), T.nt2[:, :, 0], T.dk[:], A.add, ["nt2", "dk"], ["xdd"])
+            conv("S2", 32, ["xdd"])
+        values_new("nt2")
+        if end:
+            cp(T.nn[:], B["NB"][:, 0:256], [], ["nn"], ["NB"])
+            cp(T.LL[:].indirect(T.uso[:]), T.nn[:], ["nn", "uso"], LLK)
+            dma("Y", T.yt[2::3, :], T.LL[0::16, 0:FF], r=LLK)
+            break
+        tt(T.p4[:, :, 3], T.nt2[:, :, 0], T.dk[:], A.add, ["nt2", "dk"], ["dd"])
+        cp(T.udd[:], B["S2"][:, 32:48], [], ["udd"], ["S2"])
+
+        def rewrite(deltas=deltas):
+            cp(T.uso[:], B["S2"][:, 0:16], [], ["uso"], ["S2"])
+            cp(T.LL[:].indirect(T.uso[:]), T.nn[:], ["nn", "uso"], LLK)
+            cp(T.r3[:], T.LL[:, 0:FF].indirect(T.uro[:]), LLK + ["uro"], ["r3"])
+            deltas()
+
+        pending.extend([rewrite, book])
+    emit(g, T, ops)

@@ -4,24 +4,26 @@ from concourse.mybir import AluOpType as A, ActivationFunctionType as AF
 NR, NSUB, NROUND = 4, 4, 3
 FF = 4096
 LW = FF + 256
-SPLIT = {"plain": (64, 20), "epoch": (128, 12), "req": (48, 8), "first": (64, 16), "second": (80, 16), "afterx": (80, 8)}
+SPLIT = {"plain": (64, 20), "epoch": (128, 12), "req": (48, 8), "first": (56, 8), "second": (64, 16), "afterx": (80, 8)}
 EARLY = 2
+GORDER = (0, 2, 4, 6, 1, 3, 5, 7)
 
 F32, B16, I32, U16 = "float32", "bfloat16", "int32", "uint16"
 SCRATCH = {}
 for _t, _bufs in (
         (F32, dict(sff=[2048], LL=[LW], otf=[1024], cf=[256], ww=[8, 32], wc=[128], mx=[256], th1=[16], tha=[16], thb=[16],
-                   th3=[16, 3], thp=[16, 3], p2=[16, 2],
-                   p4=[16, 4], a2=[16, 2], cc=[16], ff=[16], fk=[16], df=[16], zz=[16], t1=[16], t2=[16], xso=[128],
-                   xro=[128], xrk=[128], xdd=[128], xhh=[128], r3=[256], nn=[256], nt=[16, 16], nt2=[16, 16], idf=[128],
-                   nid=[128], idm=[128], onf=[128], z16=[32], gm=[8], col=[16], kmin=[128], selr=[8, 3], seld=[8, 2],
-                   coef=[2], dmt=[16], dml=[16], hr=[16], oh=[64], ua=[64], ub=[64], osv=[64], dk=[16], rp0=[64], rp1=[64],
-                   rp2=[64], ro0=[48], ro1=[48], ro2=[48], rg=[1024], xf=[256], ycf=[16])),
+                   th3=[16, 3], thp=[16, 3], p2=[16, 2], a2=[16, 2], cc=[16], fk=[16], df=[16], zz=[16], t1=[16], t2=[16],
+                   xso=[128], xro=[128], xdd=[128], xhh=[128], nn=[256], idf=[128], sel0=[8], ans=[16], onf=[128], z16=[32],
+                   gm=[8], col=[16], kmin=[128], coef=[2], dmt=[16], hr=[16], oh=[64], ua=[64], ub=[64], osv=[64], dk=[16],
+                   rp0=[64], rp1=[64], rp2=[64], ro0=[48], ro1=[48], ro2=[48], rg=[1024], xf=[256], ycf=[16])),
         (B16, dict(pwn=[FF], pw2=[2 * FF], xx0=[512], xx1=[512], drs=[256], xb=[2048], gg=[4096], sg=[256], hwa=[4, 8],
                    hwb=[4, 8, 2], ge=[128], cn=[256], nu=[128], fl0=[16, 5], fl1=[16, 5], xxo=[128], fat=[16, 16],
-                   fbt=[16, 16], fan=[256], fao=[256], fbn=[256], eq=[8, 384], idb=[128], id8=[128], trb=[128], trp=[128],
+                   fbt=[16, 16], fan=[256], fao=[256], fbn=[256], eq=[8, 3, 128], idb=[128], id8=[128], trp=[128],
                    onb=[128], zb=[64], z16b=[32], k01=[128], plb=[16], c256=[16], wh=[64], srv=[16])),
-        (I32, dict(sfw=[2048], oti=[1024], c0i=[16], thi=[16], fi=[16], fj=[16], dig=[16, 3], ia=[16], ib=[16], ic=[16])),
+        ("float16", dict(r3=[256], nt=[16, 16], nt2=[16, 16], idh=[128], idm=[128], nih=[128], p4=[16, 4], selr=[8, 3],
+                         seld=[8, 2])),
+        (I32, dict(sfw=[2048], oti=[1024], c0i=[16], thi=[16], ff=[16], fi=[16], fj=[16], dig=[16, 3], ia=[16], ib=[16],
+                   ic=[16])),
         (U16, dict(cu=[256], uso=[16], uro=[16], uxo=[16], udd=[16], xl=[2], rq0=[64], rq1=[64], rq2=[64]))):
     for _k in _bufs:
         SCRATCH[_k] = ("sbuf", [128] + _bufs[_k], _t)
@@ -146,17 +148,13 @@ def rank_program(g, core, T, topo):
     B = {k: T["b%d" % i] for i, k in enumerate(["V0", "V1", "CT", "NB", "EA", "EB", "S1", "S2"])}
     XL = T.xl[:, 0:1]
 
-    def conv(bk, c0, xs, base=None):
-        lo = xs[0] == "xxo"
-        z = T.z16b if lo else T.z16
+    def conv(bk, c0, x, base=False):
+        z = T.z16b if x == "xxo" else T.z16
         if base:
-            mm(B[bk][:, c0:c0 + 16], (T.idb if lo else T.idf)[:], T[base][:], True, False, [base], [bk])
+            mm(B[bk][:, c0:c0 + 16], T.idb[:], T.plb[:], True, False, ["plb"], [bk])
         for qd in range(4):
-            for n, x in enumerate(xs):
-                mm(B[bk][32 * qd:32 * qd + 32, c0:c0 + 16], z[:, 0:32], T[x][:, 32 * qd + 16:32 * qd + 32],
-                   not base and n == 0, False, [x], [bk])
-                mm(B[bk][32 * qd:32 * qd + 16, c0:c0 + 16], z[:, 16:32], T[x][:, 32 * qd:32 * qd + 16], False,
-                   n == len(xs) - 1, [x], [bk])
+            mm(B[bk][32 * qd:32 * qd + 32, c0:c0 + 16], z[:, 0:32], T[x][:, 32 * qd + 16:32 * qd + 32], not base, False, [x], [bk])
+            mm(B[bk][32 * qd:32 * qd + 16, c0:c0 + 16], z[:, 16:32], T[x][:, 32 * qd:32 * qd + 16], False, True, [x], [bk])
 
     dma("Y", T.c0i[:], T.c0[:], w=["c0i"])
     dma("S", T.xx0[:, 0:256], T.x0[:], w=["xc0"])
@@ -181,7 +179,7 @@ def rank_program(g, core, T, topo):
     remote([RemoteDMATransfer(dst_ids=[dst[r] for r in peers], dma_engine_mask=bits(eng), remote_sem=T.sem.hwin,
                               srcs=[T.hwa[:, me, 0:2]], dsts=[T.hwa[:, me, 0:2] for r in peers])], ne, ["hwo"])
     arrive("hwin", 3 * ne, ["hwr"])
-    for n, x in enumerate((T.xso, T.xro, T.xrk, T.xdd, T.xhh, T.xxo)):
+    for n, x in enumerate((T.xso, T.xro, T.xdd, T.xhh, T.xxo)):
         ms(x[:], 0.0, ["x0s%d" % n])
     ms(T.z16[:, 0:16], 0.0, ["z0"])
     ts(T.fi[:], T.ia[:], 15, A.bitwise_and, ["ia"], ["fi"])
@@ -207,11 +205,11 @@ def rank_program(g, core, T, topo):
     op("P", None, ["z0", "z1", "z16b", "idb", "idf"])
     ms(B["V1"][:, 0:256], 0.0, [], ["V1"])
     cp(T.udd[:], T.c0i[:], ["c0i"], ["udd"])
-    op("V", None, ["xl", "x0s5"])
+    op("V", None, ["xl", "x0s4"])
     cp(T.xdd[:].indirect(XL), T.c0i[:], ["c0i"], ["xdd"])
-    conv("S2", 0, ["xdd"])
+    conv("S2", 0, "xdd")
     cp(T.xro[:].indirect(XL), T.thi[:], ["thi"], ["xro"])
-    conv("S1", 0, ["xro"])
+    conv("S1", 0, "xro")
 
     def spread_x(x, xk):
         for g8 in range(8):
@@ -240,18 +238,15 @@ def rank_program(g, core, T, topo):
         ts(T.th3[:, :, s], B["S1"][:, 0:16], 1.0 / 32, A.mult, [], ["th3"], b=["S1"])
     ts(T.thb[:], B["S1"][:, 0:16], 1.0 / 32, A.mult, [], ["thb"], b=["S1"])
     ts(T.th1[:], B["S1"][:, 0:16], 1.0 / 32, A.mult, [], ["th1"], 1.0, A.add, b=["S1"])
-    act(T.nid[:], T.idf[:], AF.Copy, ["idf"], ["nid"], scale=-1.0)
+    ts(T.nih[:], T.idb[:], -1.0, A.mult, ["idb"], ["nih"])
+    cp(T.idh[:], T.idb[:], ["idb"], ["idh"])
     act(T.id8[:], T.idb[:], AF.Copy, ["idb"], ["id8"], scale=-8.0)
     tt(T.coef[:, 0:1], T.z16[:, 17:18], T.z16[:, 16:17], A.subtract, ["z1"], ["cf0"])
     tt(T.coef[:, 1:2], T.z16[:, 17:18], T.z16[:, 18:19], A.subtract, ["z1"], ["cf1"])
-    ts(T.col[:, 6:7], T.z16[:, 16:17], -1.0, A.mult, ["z1"], ["colD"], 1.0, A.add)
+    ts(T.sel0[:], T.gm[:], T.z16[:, 18:19], A.mult, ["z1", "gm"], ["sel0"])
     tt(T.thp[:], T.fl1[:, :, 2:5], T.th3[:], A.mult, ["fl1", "th3"], ["thp"])
-    ts(T.dml[:], T.plb[:], float(FF), A.add, ["plb"], ["dml"])
-    ts(T.trb[:], T.trp[:], 64.0, A.mult, ["trp"], ["trb"], -64.0, A.add)
     for g8 in range(8):
-        act(T.selr[:, g8, :], T.z16[:, 16:19], AF.Copy, ["z1", "gm"], ["selr"], scale=T.gm[:, g8:g8 + 1])
-        act(T.seld[:, g8, :], T.coef[:], AF.Copy, ["cf0", "cf1"], ["seld"], scale=T.gm[:, g8:g8 + 1])
-    act(T.idm[:], T.idf[:], AF.Copy, ["idf", "colD"], ["idm"], scale=T.col[:, 6:7])
+        ts(T.selr[:, g8, :], T.z16[:, 16:19], T.gm[:, g8:g8 + 1], A.mult, ["z1", "gm"], ["selr"])
     ms(T.nt2[:], 0.0, ["nt2"])
     cp(T.cu[:], T.sfw[:].indirect(T.udd[:]), ["sf", "udd"], ["cu"])
     cp(T.sff[:], T.sfw[:], ["sf"], ["sff"])
@@ -269,37 +264,44 @@ def rank_program(g, core, T, topo):
         if part != 1:
             mm(nb[:, 0:16], T.idb[:], T.zb[:, 0:16], True, False, ["zb"], ["S1"])
             mm(nb[:, 0:8], T.id8[:], av(0, 8), False, False, ["id8", ak[0]], ["S1"])
-            for g8 in range(8):
-                mm(nb[:, g8:g8 + 1], T.eq[:, g8, 0:128], av(g8, g8 + 1), False, False, ["eq%d" % g8], ["S1"])
-                mm(nb[:, 8 + g8:9 + g8], T.eq[:, g8, 128:256], av(g8, g8 + 1), False, False, ["eq%d" % g8, ak[0]], ["S1"])
+            for g8 in GORDER:
+                mm(nb[:, g8:g8 + 1], T.eq[:, g8, 0, :], av(g8, g8 + 1), False, False, ["eq%d" % g8], ["S1"])
+                mm(nb[:, 8 + g8:9 + g8], T.eq[:, g8, 1, :], av(g8, g8 + 1), False, False, ["eq%d" % g8, ak[0]], ["S1"])
         if part != 0:
             mm(nb[:, 8:16], T.id8[:], av(8, 16), False, False, [ak[1]], ["S1"])
-            for g8 in range(8):
-                mm(nb[:, 8 + g8:9 + g8], T.eq[:, g8, 256:384], av(8 + g8, 9 + g8), False, g8 == 7, ["eq%d" % g8, ak[1]], ["S1"])
+            for g8 in GORDER:
+                mm(nb[:, 8 + g8:9 + g8], T.eq[:, g8, 2, :], av(8 + g8, 9 + g8), False, g8 == 7, ["eq%d" % g8, ak[1]], ["S1"])
 
-    def write_offsets():
+    def write_offsets(between=None):
         ts(T.zz[:], B["S1"][:, 0:16], -8.0, A.is_equal, [], ["zz"], b=["S1"])
+        if between:
+            between()
         tt(T.xso[:].indirect(XL), T.zz[:], T.df[:], A.mult, ["zz", "df"], ["xso"])
-        conv("S2", 0, ["xso"], "dml")
+        conv("S2", 0, "xso", True)
 
-    def values_old(idm):
-        mm(B["NB"][:, 0:256], T[idm][:], T.r3[:], True, False, ["r3", idm], ["NB"])
+    def take_offsets():
+        ts(T.uso[:], B["S2"][:, 0:16], float(FF), A.add, [], ["uso"], b=["S2"])
 
-    def values_new(nt):
+    def values():
+        act(T.nn[:], B["NB"][:, 0:256], AF.Copy, [], ["nn"], ["NB"])
+
+    def values_new(nt, idm):
+        mm(B["NB"][:, 0:256], T[idm][:], T.r3[:], True, False, ["r3", "idh", idm], ["NB"])
         for h in range(2):
-            mm(B["NB"][:, 128 * h:128 * h + 128], T[nt][:, 8 * h:8 * h + 8, :], T.idf[:], False, h == 1, [nt], ["NB"])
+            mm(B["NB"][:, 128 * h:128 * h + 128], T[nt][:, 8 * h:8 * h + 8, :], T.idh[:], False, h == 1, [nt], ["NB"])
 
     def epoch_v():
-        cp(T.fi[:], T.ff[:], ["ff"], ["fi"])
-        ts(T.dig[:, :, 0], T.fi[:], 15, A.bitwise_and, ["fi"], ["dg0"])
-        ts(T.dig[:, :, 1], T.fi[:], 4, A.arith_shift_right, ["fi"], ["dg1"], 15, A.bitwise_and)
-        ts(T.dig[:, :, 2], T.fi[:], 8, A.arith_shift_right, ["fi"], ["dg2"])
+        ts(T.dig[:, :, 0], T.ff[:], 15, A.bitwise_and, ["ff"], ["dg0"])
+        ts(T.dig[:, :, 1], T.ff[:], 4, A.arith_shift_right, ["ff"], ["dg1"], 15, A.bitwise_and)
+        ts(T.dig[:, :, 2], T.ff[:], 8, A.arith_shift_right, ["ff"], ["dg2"])
         cp(T.fat[:, :, 0:3], T.dig[:], ["dg0", "dg1", "dg2", "fat"], ["fa0"])
 
-    def epoch_features():
+    def epoch_squares():
         act(T.fbt[:, :, 0:3], T.fat[:, :, 0:3], AF.Copy, ["fa0", "fbt"], ["fb0"])
         act(T.fat[:, :, 3:6], T.fat[:, :, 0:3], AF.Square, ["fa0"], ["fa1"])
         act(T.fbt[:, :, 6:9], T.fat[:, :, 0:3], AF.Square, ["fa0"], ["fb1"])
+
+    def epoch_features():
         for h in range(2):
             mm(B["EA"][:, 128 * h:128 * h + 128], T.fat[:, 8 * h:8 * h + 8, :], T.idb[:], True, True, ["fa0", "fa1"], ["EA"])
         for h in range(2):
@@ -310,16 +312,16 @@ def rank_program(g, core, T, topo):
 
     def epoch_pairs(n0, n1):
         for n in range(n0, n1):
-            g8 = (0, 2, 4, 6, 1, 3, 5, 7)[n]
+            g8 = GORDER[n]
             bk = "EB" if n % 2 == 0 else "EA"
             p0 = 32 * (g8 // 2)
             p1 = p0 + (32 if g8 % 2 else 16)
             fa = "fao" if g8 % 2 else "fan"
-            mm(B[bk][:, 0:256], T[fa][p0:p1, 0:128], T.fbn[p0:p1, 0:256], True, False, [fa, "fbn"], [bk])
-            mm(B[bk][:, 0:128], T.idb[:], T.trb[:], False, True, ["trb"], [bk])
-            mm(B[bk][:, 256:384], T[fa][p0:p1, 128:256], T.fbn[p0:p1, 128:256], True, False, [fa, "fbn"], [bk])
-            mm(B[bk][:, 256:384], T.idb[:], T.trb[:], False, True, [], [bk])
-            act(T.eq[:, g8, :], B[bk][:, 0:384], AF.Relu, ["onf"], ["eq%d" % g8], [bk], bias=T.onf[:, 0:1], scale=2.0)
+            mm(B[bk][:, 0:256], T[fa][p0:p1, 0:128], T.fbn[p0:p1, 0:256], True, True, [fa, "fbn"], [bk])
+            mm(B[bk][:, 256:384], T[fa][p0:p1, 128:256], T.fbn[p0:p1, 128:256], True, True, [fa, "fbn"], [bk])
+            act(T.eq[:, g8, :, :], B[bk][:, 0:384], AF.Relu, ["onf"], ["eq%d" % g8], [bk], bias=T.onf[:, 0:1], scale=2.0)
+            op("G", lambda e, v=T.eq[:, g8, 0::2, :]: e.affine_select(v, v, [[0, 2], [1, 128]], A.is_gt, 0.0, 0, -1),
+               ["eq%d" % g8], ["eq%d" % g8])
 
     def request_sums(xc, xk):
         for r in range(NR):
@@ -328,8 +330,7 @@ def rank_program(g, core, T, topo):
                 mm(B["S1"][:, c0:c0 + 16], xc[:, 128 * h:128 * h + 128], T.hwb[:, r, :, :], True, True, [xk, "hwb"], ["S1"])
 
     def request():
-        cp(T.fi[:], T.ff[:], ["ff"], ["fi"])
-        ts(T.fj[:], T.fi[:], 3, A.bitwise_and, ["fi"], ["fj"])
+        ts(T.fj[:], T.ff[:], 3, A.bitwise_and, ["ff"], ["fj"])
         for r in range(NR):
             ts(T.oh[:, 16 * r:16 * r + 16], T.fj[:], float(r), A.is_equal, ["fj"], ["oh"])
         cp(T.hr[:], T.fj[:], ["fj"], ["hr"])
@@ -355,7 +356,7 @@ def rank_program(g, core, T, topo):
             act(T.rg[:, 128 * c + 384:128 * c + 512], win.indirect(rq[:, 8 * c + 24:8 * c + 32]), AF.Copy,
                 LLK + ["rqi%d" % rnd], ["rg%d" % (c + 3)])
         for c in (2, 5, 3, 6, 4, 7):
-            mm(B["EA"][:, 8 * c:8 * c + 8], T.rg[:, 128 * c:128 * c + 128], T.selr[:, :, 2], True, True, ["rg%d" % c, "selr"], ["EA"])
+            mm(B["EA"][:, 8 * c:8 * c + 8], T.rg[:, 128 * c:128 * c + 128], T.sel0[:], True, True, ["rg%d" % c, "sel0"], ["EA"])
         act(ro[:], B["EA"][:, 16:64], AF.Copy, [], ["ro%d" % rnd], ["EA"])
         remote([RemoteDMATransfer(dst_ids=[dst[(me - s) % NR]], dma_engine_mask=bits(share[s - 1]), remote_sem=T.sem["rpin%d" % rnd],
                                   src=ro[:, 16 * s - 16:16 * s], dst=rp[:, 16 * me:16 * me + 16]) for s in range(1, NR)],
@@ -365,7 +366,7 @@ def rank_program(g, core, T, topo):
 
     def answer_own(rnd):
         for c in range(2):
-            mm(B["EB"][:, 8 * c:8 * c + 8], T.rg[:, 128 * c:128 * c + 128], T.selr[:, :, 2], True, True, ["rg0"], ["EB"])
+            mm(B["EB"][:, 8 * c:8 * c + 8], T.rg[:, 128 * c:128 * c + 128], T.sel0[:], True, True, ["rg0"], ["EB"])
         act(T["rp%d" % rnd][:, 16 * me:16 * me + 16], B["EB"][:, 0:16], AF.Copy, [], ["rpo%d" % rnd], ["EB"])
 
     def planes(q, a, b):
@@ -397,14 +398,12 @@ def rank_program(g, core, T, topo):
             cp(T.wc[:], WW, ["ww"], ["wc"])
         scan(T.cn[:, 128 * h:128 * h + 128], T.k01[:], T.ge[:], A.mult, A.add, ["ge", "k01"], ["cn%d" % h])
         c, cnt = slice(8 * h, 8 * h + 8), T.cn[:, 128 * h + 15:128 * h + 128:16]
-        if not h:
-            least_a()
+        scan(MS, T.kmin[:], T.wc[:], A.add, A.min, ["wc", "kmin"], ["ms"], ["CT"])
         if swaps:
             tt(fl[:, c, 0], cnt, T.tha[:, c], A.is_ge, ["cn%d" % h, "tha"], [fk + "a%d" % h])
+        if not h:
+            least_b()
         tt(fl[:, c, 4], cnt, T.thb[:, c], A.is_ge, ["cn%d" % h, "thb"], [fk + "b%d" % h])
-
-    def least_a():
-        scan(MS, T.kmin[:], T.wc[:], A.add, A.min, ["wc", "kmin"], ["ms"], ["CT"])
 
     def least_b():
         tt(T.nu[:], MS, T.wc[:], A.not_equal, ["ms", "wc"], ["nu"], ["CT"])
@@ -412,7 +411,17 @@ def rank_program(g, core, T, topo):
     def least_c(h):
         scan(T.mx[:, 128 * h:128 * h + 128], T.nu[:], B["CT"][:, 128 * h:128 * h + 128], A.mult, A.max, ["nu"], ["mx%d" % h], ["CT"])
 
-    pending = []
+    def weave(fns):
+        segs = []
+        for fn in fns:
+            n = len(ops)
+            fn()
+            segs.append(ops[n:])
+            del ops[n:]
+        for k in range(max([len(x) for x in segs] + [0])):
+            ops.extend(x[k] for x in segs if k < len(x))
+
+    first, pending = [], []
     NT = NSUB * NROUND
     for t in range(NT):
         rnd, last_sub, end = t // NSUB, t % NSUB == NSUB - 1, t == NT - 1
@@ -430,88 +439,99 @@ def rank_program(g, core, T, topo):
             cp(T.cu[:], T.sfw[:].indirect(T.udd[:]), ["sf", "udd"], ["cu"])
         act(T.cf[:], T.sff[:].indirect(T.udd[:]), AF.Identity, ["sff", "udd", "colC"], ["cf"], bias=T.col[:, 5:6])
         if kind == "afterx":
-            act(T.nn[:], B["NB"][:, 0:256], AF.Copy, [], ["nn"], ["NB"])
+            values()
             write_offsets()
         if last_sub:
             request_sums(xc, xck)
         if epoch:
             epoch_pairs(EARLY if kind == "afterx" else 0, 8)
+        mm(B["EB"][:, 0:256], T.idb[:], xc[:, 0:256], True, False, [xck], ["EB"])
+        mm(B["EB"][:, 0:256], T.idb[:], T.drs[:], False, True, ["dr"], ["EB"])
         planes("S", a0, 128)
         m1 = (a1 + 256) // 4 * 2
         m2 = (m1 + 256) // 4 * 2
-        planes("S", a1, m1)
-        planes("S", m1, m2)
-        planes("S", m2, 256)
+        m3 = (m2 + 256) // 4 * 2
+        for a, b in ((a1, m1), (m1, m2), (m2, m3), (m3, 256)):
+            planes("S", a, b)
         planes("V", 0, a0 // 2)
         for h in range(2):
             op("P", lambda e, h=h: e.transpose(B["CT"][:, 128 * h:128 * h + 128], T.cf[:, 128 * h:128 * h + 128], T.idf[:]),
                ["cf"], [], ["CT"])
-        mm(B["EB"][:, 0:256], T.idb[:], xc[:, 0:256], True, False, [xck], ["EB"])
-        mm(B["EB"][:, 0:256], T.idb[:], T.drs[:], False, True, ["dr"], ["EB"])
         dots(0, a0 // 2)
         if t == 0:
             cp(T.otf[0:96, :], T.oti[0:96, :], ["oti0", "oti1", "oti2"], ["otf"])
             for k in range(3):
                 dma("Y", T.LL[2 - k::16, 0:FF], T.otf[32 * k:32 * k + 32, :], r=["otf", "LLz"], w=["LL%d" % k])
         if t == 1:
+            ts(T.col[:, 6:7], T.z16[:, 16:17], -1.0, A.mult, ["z1"], ["colD"], 1.0, A.add)
+            for g8 in range(8):
+                ts(T.seld[:, g8, :], T.coef[:], T.gm[:, g8:g8 + 1], A.mult, ["cf0", "cf1"], ["seld"])
+            ts(T.idm[:], T.idb[:], T.col[:, 6:7], A.mult, ["colD"], ["idm"])
             for g8 in range(8):
                 ts(T.hwb[:, :, g8, :], T.hwa[:, :, 0:2], T.gm[:, g8:g8 + 1], A.mult, ["hwo", "hwr", "gm"], ["hwb"])
-        for fn in pending:
-            fn()
-        del pending[:]
         if last_sub:
-            request()
+            pending.append(request)
+        for fn in first:
+            fn()
+        weave(pending)
+        del first[:], pending[:]
         dots(a0, 128)
         if last_sub:
-            conv("S2", 16, ["xhh"])
+            conv("S2", 16, "xhh")
         planes("V", a0 // 2, a0)
         if last_sub:
             request_send(rnd)
         planes("V", 128, a1)
         dots(a0 // 2, a0)
         if swaps:
-            values_old("idf")
-            values_new("nt")
+            values_new("nt", "idh")
         dots(128, 256)
+        act(T.sg[:], B["EB"][:, 0:256], AF.Sign, ["colE"], ["sg"], ["EB"], bias=T.col[:, 7:8])
         test(0, fl, fk, swaps)
-        least_b()
         least_c(0)
         av = lambda a, b, fl=fl: fl[:, a:b, 0]
         if swaps:
             blockers(av, [fk + "a0", fk + "a1"], 0)
-        act(T.sg[:], B["EB"][:, 0:256], AF.Sign, ["colE"], ["sg"], ["EB"], bias=T.col[:, 7:8])
+        test(1, fl, fk, swaps)
+        if swaps:
+            values()
+            blockers(av, [fk + "a0", fk + "a1"], 1)
+        least_b()
+        tt(T.xxo[:].indirect(XL), fl[:, :, 4], T.c256[:], A.mult, FK[1:] + ["c256"], ["xxo"])
+        conv("V1", 256, "xxo", True)
+        if swaps:
+            write_offsets(lambda: least_c(1))
+        else:
+            least_c(1)
         mm(B["EA"][:, 0:256], T.idb[:], xc[:, 0:256], True, False, [xck], ["EA"])
         mm(B["EA"][:, 0:256], T.idb[:], T.drs[:], False, False, [], ["EA"])
         mm(B["EA"][:, 0:256], T.id8[:], T.sg[:], False, True, ["sg", "id8"], ["EA"])
-        test(1, fl, fk, swaps)
-        if swaps:
-            act(T.nn[:], B["NB"][:, 0:256], AF.Copy, [], ["nn"], ["NB"])
-            blockers(av, [fk + "a0", fk + "a1"], 1)
         act(xc[:, 256:512], B["EA"][:, 0:256], AF.Identity, ["colF"], [xk1], ["EA"], bias=T.col[:, 8:9])
-        least_a()
-        tt(T.xxo[:].indirect(XL), fl[:, :, 4], T.c256[:], A.mult, FK[1:] + ["c256"], ["xxo"])
-        conv("V1", 256, ["xxo"], "plb")
-        if swaps:
-            write_offsets()
-        least_b()
-        least_c(1)
-
-        def new_f(fo=fo, FOK=FOK):
-            tt(T.fi[:], T.mx[:, 15::16], fo[:, :, 4], A.mult, ["mx0", "mx1"] + FOK, ["fi"])
+        if last_sub:
             cp(T.uxo[:], B["V1"][:, 256:272], [], ["uxo"], ["V1"])
-            ts(T.fj[:], T.fi[:], 8191, A.bitwise_and, ["fi"], ["fj"], 1, A.arith_shift_right)
-            if swaps and not last_sub:
-                cp(T.uso[:], B["S2"][:, 0:16], [], ["uso"], ["S2"])
-            cp(T.xro[:].indirect(XL), T.fj[:], ["fj"], ["xro"])
-            conv("V0", 256, ["xrk", "xro"])
 
-        def rows(fl=fl, fk=fk):
-            for s in range(3):
+        def rows(s0, s1):
+            for s in range(s0, s1):
                 tt(fl[:, :, 1 + s], CNT, T.thp[:, :, s], A.is_lt, ["cn0", "cn1", "thp"], [fk])
+
+        def new_f():
+            tt(T.fi[:], T.mx[:, 15::16], fo[:, :, 4], A.mult, ["mx0", "mx1"] + FOK, ["fi"])
+            if last_sub:
+                rows(1, 2)
+            else:
+                cp(T.uxo[:], B["V1"][:, 256:272], [], ["uxo"], ["V1"])
+            ts(T.fj[:], T.fi[:], 8191, A.bitwise_and, ["fi"], ["fj"], 1, A.arith_shift_right)
+            rows(0, 1)
             tt(T.ff[:], T.fj[:], T.fk[:], A.add, ["fj", "fk"], ["ff"])
+            if last_sub:
+                rows(2, 3)
+            elif swaps:
+                take_offsets()
+            cp(T.xro[:].indirect(XL), T.ff[:], ["ff"], ["xro"])
+            conv("V0", 256, "xro")
 
         if last_sub:
-            cp(T.uso[:], B["S2"][:, 0:16], [], ["uso"], ["S2"])
+            take_offsets()
         else:
             new_f()
         if swaps:
@@ -531,9 +551,8 @@ def rank_program(g, core, T, topo):
                 spread_x(xn, xnk)
             mm(B["S1"][:, 16:64], T.idb[:], T.zb[:, 0:48], True, False, ["zb"], ["S1"])
             for s in range(3):
-                mm(B["S1"][:, 16 + s:64:3], T.nid[:], T.p4[:, :, 3], False, False, ["nid", "dd"], ["S1"])
+                mm(B["S1"][:, 16 + s:64:3], T.nih[:], T.p4[:, :, 3], False, False, ["nih", "dd"], ["S1"])
         if last_sub:
-            rows()
             tt(T.p2[:], fl[:, :, 1:4:2], fl[:, :, 2:5:2], A.add, FK, ["p2"])
             tt(T.t1[:], T.p2[:, :, 0], T.p2[:, :, 1], A.add, ["p2"], ["t1"])
         cp(T.uro[:], B["V0"][:, 256:272], [], ["uro"], ["V0"])
@@ -542,7 +561,7 @@ def rank_program(g, core, T, topo):
             for h in range(2):
                 mm(B["S1"][:, 16 + 24 * h:40 + 24 * h], T.r3[:, 128 * h:128 * h + 128], T.selr[:], False, h == 1, ["r3", "selr"], ["S1"])
         if not last_sub:
-            rows()
+            rows(1, 3)
         else:
             ts(T.t2[:], T.t1[:], 8.0, A.mult, ["t1"], ["t2"])
             tt(T.t1[:], T.t2[:], T.hr[:], A.add, ["t2", "hr"], ["t1"])
@@ -552,9 +571,11 @@ def rank_program(g, core, T, topo):
             tt(T.p4[:, :, 0:3], B["S1"][:, 16:64], fl[:, :, 1:4], A.mult, FK, ["p4"], ["S1"])
             tt(T.a2[:], T.p4[:, :, 0:2], T.p4[:, :, 2:4], A.add, ["p4", "dd"], ["a2"])
 
-        def flags(fl=fl, FK=FK):
+        def flags_a(fl=fl, FK=FK):
             tt(T.p2[:], fl[:, :, 1:4:2], fl[:, :, 2:5:2], A.add, FK, ["p2"])
             tt(T.t2[:], fl[:, :, 4], T.ff[:], A.mult, FK + ["ff"], ["t2"])
+
+        def flags_b(fl=fl, FK=FK):
             tt(T.tha[:], T.th1[:], T.p2[:, :, 0], A.subtract, ["th1", "p2"], ["tha"])
             tt(T.thp[:], fl[:, :, 2:5], T.th3[:], A.mult, FK, ["thp"])
             tt(T.thb[:], T.tha[:], T.p2[:, :, 1], A.subtract, ["tha", "p2"], ["thb"])
@@ -565,7 +586,6 @@ def rank_program(g, core, T, topo):
 
         def book(fl=fl, FK=FK, t=t):
             tt(T.fk[:], T.ff[:], T.t2[:], A.subtract, ["ff", "t2"], ["fk"])
-            tt(T.xrk[:].indirect(XL), T.ff[:], T.t2[:], A.subtract, ["ff", "t2"], ["xrk"])
             if t >= 1:
                 tt(T.nt[:, :, 0:3:2], B["S1"][:, 64:96], fl[:, :, 1:3], A.mult, FK, ["nt"], ["S1"])
                 tt(T.t1[:], T.nt[:, :, 0], T.nt[:, :, 2], A.add, ["nt"], ["t1"])
@@ -579,27 +599,28 @@ def rank_program(g, core, T, topo):
 
         if not last_sub:
             tt(T.xdd[:].indirect(XL), T.a2[:, :, 0], T.a2[:, :, 1], A.add, ["a2"], ["xdd"])
-            conv("S2", 0, ["xdd"])
+            conv("S2", 0, "xdd")
             if t >= 1:
                 deltas()
             tt(T.p4[:, :, 3], T.a2[:, :, 0], T.a2[:, :, 1], A.add, ["a2"], ["dd"])
             if t % 2:
                 epoch_v()
+                epoch_squares()
                 epoch_features()
-                pending.append(flags)
+                first.append(flags_a)
             else:
-                flags()
+                flags_a()
             cp(T.udd[:], B["S2"][:, 0:16], [], ["udd"], ["S2"])
-            pending.extend([book, cells])
+            pending.extend([flags_b, book, cells])
             continue
         rp = T["rp%d" % rnd]
         mm(B["S1"][:, 128:192], T.trp[:], T.wh[:], True, False, ["wh", "trp"], ["S1"])
         for r in range(NR):
             mm(B["S1"][:, 136 + 16 * r:144 + 16 * r], T.onb[:], T.wh[:, 16 * r:16 * r + 8], False, r == NR - 1, ["wh", "onb"], ["S1"])
-        values_old("idm")
         if not end:
             tt(T.p4[:, :, 3], T.a2[:, :, 0], T.a2[:, :, 1], A.add, ["a2"], ["dd"])
             epoch_v()
+            epoch_squares()
             spread_x(xn, xnk)
             epoch_features()
         ts(T.ua[:], B["S1"][:, 128:192], 32.0, A.is_lt, [], ["ua"], b=["S1"])
@@ -611,8 +632,8 @@ def rank_program(g, core, T, topo):
         if end:
             cp(T.xro[:].indirect(XL), T.cc[:], ["cc"], ["xro"])
             write_offsets()
-            conv("V0", 256, ["xro"])
-            cp(T.uso[:], B["S2"][:, 0:16], [], ["uso"], ["S2"])
+            conv("V0", 256, "xro")
+            take_offsets()
             cp(T.ycf[:], B["V0"][:, 256:272], [], ["ycf"], ["V0"])
             dma("Y", T.yc[:], T.ycf[:], r=["ycf"])
         else:
@@ -620,27 +641,30 @@ def rank_program(g, core, T, topo):
             tt(fl[:, :, 1], fl[:, :, 1], T.srv[:], A.add, FK + ["srv"], [fk])
             tt(T.dk[:], T.p4[:, :, 3], T.t1[:], A.subtract, ["t1", "dd"], ["dk"])
             epoch_pairs(0, EARLY)
-            flags()
+            flags_a()
+            flags_b()
         tt(T.ub[:], rp[:], T.osv[:], A.mult, ["rpi%d" % rnd, "rpo%d" % rnd, "osv"], ["ub"])
         tt(T.ua[:, 0:32], T.ub[:, 0:32], T.ub[:, 32:64], A.add, ["ub"], ["ua"])
-        tt(T.nt2[:, :, 0], T.ua[:, 0:16], T.ua[:, 16:32], A.add, ["ua"], ["nt2"])
         if not end:
-            tt(T.xdd[:].indirect(XL), T.nt2[:, :, 0], T.dk[:], A.add, ["nt2", "dk"], ["xdd"])
-            conv("S2", 32, ["xdd"])
-        values_new("nt2")
+            tt(T.ans[:], T.ua[:, 0:16], T.ua[:, 16:32], A.add, ["ua"], ["ans"])
+            tt(T.xdd[:].indirect(XL), T.ans[:], T.dk[:], A.add, ["ans", "dk"], ["xdd"])
+            conv("S2", 32, "xdd")
+        tt(T.nt2[:, :, 0], T.ua[:, 0:16], T.ua[:, 16:32], A.add, ["ua"], ["nt2"])
+        values_new("nt2", "idm")
         if end:
             cp(T.nn[:], B["NB"][:, 0:256], [], ["nn"], ["NB"])
             cp(T.LL[:].indirect(T.uso[:]), T.nn[:], ["nn", "uso"], LLK)
             dma("Y", T.yt[2::3, :], T.LL[0::16, 0:FF], r=LLK)
             break
-        tt(T.p4[:, :, 3], T.nt2[:, :, 0], T.dk[:], A.add, ["nt2", "dk"], ["dd"])
+        tt(T.p4[:, :, 3], T.ans[:], T.dk[:], A.add, ["ans", "dk"], ["dd"])
         cp(T.udd[:], B["S2"][:, 32:48], [], ["udd"], ["S2"])
 
         def rewrite(deltas=deltas):
-            cp(T.uso[:], B["S2"][:, 0:16], [], ["uso"], ["S2"])
+            take_offsets()
             cp(T.LL[:].indirect(T.uso[:]), T.nn[:], ["nn", "uso"], LLK)
             cp(T.r3[:], T.LL[:, 0:FF].indirect(T.uro[:]), LLK + ["uro"], ["r3"])
             deltas()
 
-        pending.extend([rewrite, book])
+        first.append(rewrite)
+        pending.append(book)
     emit(g, T, ops)

from concourse.bass import DstId, RemoteDMATransfer
from concourse.mybir import AluOpType as A, ActivationFunctionType as AF

NR, NSUB, NROUND = 4, 4, 3
FF = 4096
LW = FF + 256
SPLIT = {"plain": (64, 20), "epoch": (128, 12), "req": (48, 8), "first": (56, 8), "second": (64, 16), "afterx": (80, 8)}
EARLY = 2
GORDER = (0, 2, 4, 6, 1, 3, 5, 7)

F32, B16, I32, U16 = "float32", "bfloat16", "int32", "uint16"
SCRATCH = {}
for _t, _bufs in (
        (F32, dict(sff=[2048], LL=[LW], otf=[1024], cf=[256], ww=[8, 32], wc=[128], mx=[256], th1=[16], tha=[16], thb=[16],
                   th3=[16, 3], thp=[16, 3], p2=[16, 2], a2=[16, 2], cc=[16], fk=[16], df=[16], zz=[16], t1=[16], t2=[16],
                   xso=[128], xro=[128], xdd=[128], xhh=[128], nn=[256], idf=[128], sel0=[8], ans=[16], onf=[128], z16=[32],
                   gm=[8], col=[16], kmin=[128], coef=[2], dmt=[16], hr=[16], oh=[64], ua=[64], ub=[64], osv=[64], dk=[16],
                   rp0=[64], rp1=[64], rp2=[64], ro0=[48], ro1=[48], ro2=[48], rg=[1024], xf=[256], ycf=[16])),
        (B16, dict(pwn=[FF], pw2=[2 * FF], xx0=[512], xx1=[512], drs=[256], xb=[2048], gg=[4096], sg=[256], hwa=[4, 8],
                   hwb=[4, 8, 2], ge=[128], cn=[256], nu=[128], fl0=[16, 5], fl1=[16, 5], xxo=[128], fat=[16, 16],
                   fbt=[16, 16], fan=[256], fao=[256], fbn=[256], eq=[8, 3, 128], idb=[128], id8=[128], trp=[128],
                   onb=[128], zb=[64], z16b=[32], k01=[128], plb=[16], c256=[16], wh=[64], srv=[16])),
        ("float16", dict(r3=[256], nt=[16, 16], nt2=[16, 16], idh=[128], idm=[128], nih=[128], p4=[16, 4], selr=[8, 3],
                         seld=[8, 2])),
        (I32, dict(sfw=[2048], oti=[1024], c0i=[16], thi=[16], ff=[16], fi=[16], fj=[16], dig=[16, 3], ia=[16], ib=[16],
                   ic=[16])),
        (U16, dict(cu=[256], uso=[16], uro=[16], uxo=[16], udd=[16], xl=[2], rq0=[64], rq1=[64], rq2=[64]))):
    for _k in _bufs:
        SCRATCH[_k] = ("sbuf", [128] + _bufs[_k], _t)
for _i in range(8):
    SCRATCH["b%d" % _i] = ("psum", [128, 512], F32)
SEMAPHORES = ["qV", "qS", "qP", "qG", "sent", "hwin"] + ["d%d" % i for i in range(32)] + \
    ["rqin%d" % i for i in range(3)] + ["rpin%d" % i for i in range(3)]


def emit(g, T, ops):
    Q = {"V": g.vector, "S": g.scalar, "P": g.tensor, "G": g, "Y": g.sync}
    lastw, readers, bank = {}, {}, {}
    seen = {q: {} for q in Q}
    for i, o in enumerate(ops):
        q = o["q"]
        deps = set((lastw[k], True) for k in o["r"] if k in lastw)
        for k in o["w"]:
            if k in lastw:
                deps.add((lastw[k], False))
            deps.update((j, False) for j in readers.get(k, []))
        for k in o["b"]:
            deps.update((j, False) for j in bank.setdefault(k, {}).values())
            bank[k][q] = i
        need = {}
        for j, raw in deps:
            p = ops[j]
            if p["tok"] is not None:
                need[("tok", j)] = j
            elif p["q"] != q or raw:
                need[p["q"]] = max(need.get(p["q"], -1), j)
        o["waits"] = []
        for k in sorted(need, key=str):
            j = need[k]
            if seen[q].get(k, -1) < j:
                seen[q][k] = j
                o["waits"].append(j)
                ops[j]["inc"] = True
        for k in o["r"]:
            readers.setdefault(k, []).append(i)
        for k in o["w"]:
            lastw[k] = i
            readers[k] = []
    cnt = {q: 0 for q in Q}
    last = {}
    for o in ops:
        if o["tok"] is not None:
            o["val"] = last[o["tname"]] = o["tok"]
        elif o["inc"]:
            cnt[o["q"]] += 1
            o["val"] = (T.sem["q" + o["q"]], cnt[o["q"]])
    for o in ops:
        e = Q[o["q"]]
        for j in o["waits"]:
            e.wait_ge(*ops[j]["val"])
        if o["fn"] is None:
            continue
        ins = o["fn"](e)
        if o["dma"]:
            ins.then_inc(o["tok"][0], 16)
        elif o["tok"] is None and o["inc"]:
            ins.then_inc(o["val"][0], 1)
    for k in last:
        g.sync.wait_ge(*last[k])


def rank_program(g, core, T, topo):
    me = T.rank_of(core)
    if me is None:
        return
    ops = []
    nd = [0]
    sent = [0]

    def op(q, fn, r=(), w=(), b=(), tname=None, val=0, isdma=False):
        ops.append(dict(q=q, fn=fn, r=list(r), w=list(w), b=list(b), tok=(T.sem[tname], val) if tname else None,
                        tname=tname, inc=False, dma=isdma))

    def dma(q, out, in_, r=(), w=()):
        nd[0] += 1
        op(q, lambda e: e.dma_start(out, in_), r, w, (), "d%d" % (nd[0] - 1), 16, True)

    def arrive(name, val, w):
        op("G", None, (), w, (), name, val)

    def remote(trs, n, r):
        sent[0] += n
        op("G", lambda e: e.remote_dma_fused(trs, local_sem=T.sem.sent), r, (), (), "sent", sent[0])

    def cp(out, in_, r, w, b=()):
        op("V", lambda e: e.tensor_copy(out, in_), r, w, b)

    def tt(out, a, c, o, r, w, b=()):
        op("V", lambda e: e.tensor_tensor(out, a, c, o), r, w, b)

    def ts(out, a, s1, o0, r, w, s2=None, o1=None, b=()):
        if o1 is None:
            op("V", lambda e: e.tensor_scalar(out, a, s1, None, o0), r, w, b)
        else:
            op("V", lambda e: e.tensor_scalar(out, a, s1, s2, o0, o1), r, w, b)

    def scan(out, d0, d1, o0, o1, r, w, b=()):
        op("V", lambda e: e.tensor_tensor_scan(out, d0, d1, 0.0, o0, o1), r, w, b)

    def ms(ap, v, w, b=()):
        op("V", lambda e: e.memset(ap, v), w, w, b)

    def act(out, in_, f, r, w, b=(), **kw):
        op("S", lambda e: e.activation(out, in_, f, **kw), r, w, b)

    def mm(out, l, rr, st, sp, r, b):
        op("P", lambda e: e.matmul(out, l, rr, st, sp), r, (), b)

    peers = [(me + s) % NR for s in range(1, NR)]
    dst = {}
    for r in peers:
        rid, pid, _ = topo.addr(T.cores[r])
        dst[r] = DstId(rid=rid, pnc=pid)
    eng = [e for e in topo.engines(core, T.cores[peers[0]]) if all(e in topo.engines(core, T.cores[r]) for r in peers)]
    ne = len(eng)
    bits = lambda es: sum(1 << e for e in es)
    share = [eng[:ne // 2], eng[ne // 2:3 * ne // 4], eng[3 * ne // 4:]]
    B = {k: T["b%d" % i] for i, k in enumerate(["V0", "V1", "CT", "NB", "EA", "EB", "S1", "S2"])}
    XL = T.xl[:, 0:1]

    def conv(bk, c0, x, base=False):
        z = T.z16b if x == "xxo" else T.z16
        if base:
            mm(B[bk][:, c0:c0 + 16], T.idb[:], T.plb[:], True, False, ["plb"], [bk])
        for qd in range(4):
            mm(B[bk][32 * qd:32 * qd + 32, c0:c0 + 16], z[:, 0:32], T[x][:, 32 * qd + 16:32 * qd + 32], not base, False, [x], [bk])
            mm(B[bk][32 * qd:32 * qd + 16, c0:c0 + 16], z[:, 16:32], T[x][:, 32 * qd:32 * qd + 16], False, True, [x], [bk])

    dma("Y", T.c0i[:], T.c0[:], w=["c0i"])
    dma("S", T.xx0[:, 0:256], T.x0[:], w=["xc0"])
    dma("Y", T.thi[:], T.th[:], w=["thi"])
    dma("S", T.hwa[:, me, 0:2], T.hw[:], w=["hwo"])
    dma("Y", T.sfw[:], T.sf[:], w=["sf"])
    for k in range(4):
        dma("Y", T.pwn[:, 1024 * k:1024 * k + 1024], T.pw[:, 1024 * k:1024 * k + 1024], w=["pw%d" % k])
    dma("Y", T.drs[:], T.dr[:], w=["dr"])
    for k in range(3):
        dma("Y", T.oti[32 * k:32 * k + 32, :], T.ot[k::3, :], w=["oti%d" % k])

    ms(T.onf[:], 1.0, ["onf"])
    ms(T.onb[:], 1.0, ["onb"])
    op("G", lambda e: e.iota(T.ia[:], [[-1, 16]], 0, 1), (), ["ia"])
    op("G", lambda e: e.iota(T.ib[:, 0:8], [[-16, 8]], 0, 1), (), ["ib"])
    op("G", lambda e: e.iota(T.ic[:], [[16, 16]], 0, 1), (), ["ic"])
    op("G", lambda e: e.affine_select(T.idf[:], T.onf[:], [[-1, 128]], A.is_equal, 0.0, 0, 1), ["onf"], ["idf"])
    op("G", lambda e: e.iota(T.dmt[:], [[128, 2], [0, 8]], FF, 1, allow_small_or_imprecise_dtypes=True), (), ["dmt"])
    op("G", lambda e: e.affine_select(T.trp[:], T.onb[:], [[1, 128]], A.is_gt, 0.0, 0, -1), ["onb"], ["trp"])
    op("G", lambda e: e.iota(T.LL[:], [[0, LW]], 0, 0, allow_small_or_imprecise_dtypes=True), (), ["LLz"])
    remote([RemoteDMATransfer(dst_ids=[dst[r] for r in peers], dma_engine_mask=bits(eng), remote_sem=T.sem.hwin,
                              srcs=[T.hwa[:, me, 0:2]], dsts=[T.hwa[:, me, 0:2] for r in peers])], ne, ["hwo"])
    arrive("hwin", 3 * ne, ["hwr"])
    for n, x in enumerate((T.xso, T.xro, T.xdd, T.xhh, T.xxo)):
        ms(x[:], 0.0, ["x0s%d" % n])
    ms(T.z16[:, 0:16], 0.0, ["z0"])
    ts(T.fi[:], T.ia[:], 15, A.bitwise_and, ["ia"], ["fi"])
    ts(T.fj[:, 0:8], T.ib[:, 0:8], 4, A.arith_shift_right, ["ib"], ["fj"])
    pc = T.ic[:, 0:1]
    ts(T.dig[:, 0, 0:1], pc, 7, A.bitwise_and, ["ic"], ["dg0"])
    ts(T.dig[:, 0, 1:2], pc, 8, A.bitwise_and, ["ic"], ["dg1"])
    ts(T.dig[:, 0, 2:3], pc, 4, A.arith_shift_right, ["ic"], ["dg2"])
    ts(T.dig[:, 1, 0:1], pc, 15, A.bitwise_and, ["ic"], ["dg3"])
    ts(T.dig[:, 1, 1:2], pc, 4, A.arith_shift_right, ["ic"], ["dg4"], 1, A.bitwise_and)
    ts(T.gm[:], T.fj[:, 0:8], 0.0, A.is_equal, ["fj"], ["gm"])
    ts(T.z16[:, 16:32], T.fi[:], 0.0, A.is_equal, ["fi"], ["z1"])
    cp(T.col[:, 0:3], T.dig[:, 0, 0:3], ["dg0", "dg1", "dg2"], ["colA"])
    cp(T.col[:, 3:5], T.dig[:, 1, 0:2], ["dg3", "dg4"], ["colB"])
    ms(B["V0"][:, 0:256], 0.0, [], ["V0"])
    ts(T.t1[:, 0:1], T.col[:, 0:1], 16.0, A.mult, ["colA"], ["t1"], T.col[:, 1:2], A.add)
    ts(T.t2[:, 0:1], T.col[:, 2:3], -16.0, A.mult, ["colA"], ["t2"])
    ts(T.col[:, 5:6], T.col[:, 3:4], -8192.0, A.mult, ["colB"], ["colC"], 8192.0 * 15, A.add)
    cp(T.z16b[:], T.z16[:], ["z0", "z1"], ["z16b"])
    cp(T.idb[:], T.idf[:], ["idf"], ["idb"])
    ts(T.xl[:, 0:1], T.t1[:, 0:1], T.col[:, 2:3], A.add, ["t1", "colA"], ["xl"])
    ts(T.plb[:], T.ic[:], T.t2[:, 0:1], A.add, ["t2", "ic"], ["plb"])
    op("P", None, ["z0", "z1", "z16b", "idb", "idf"])
    ms(B["V1"][:, 0:256], 0.0, [], ["V1"])
    cp(T.udd[:], T.c0i[:], ["c0i"], ["udd"])
    op("V", None, ["xl", "x0s4"])
    cp(T.xdd[:].indirect(XL), T.c0i[:], ["c0i"], ["xdd"])
    conv("S2", 0, "xdd")
    cp(T.xro[:].indirect(XL), T.thi[:], ["thi"], ["xro"])
    conv("S1", 0, "xro")

    def spread_x(x, xk):
        for g8 in range(8):
            act(T.xb[:, 256 * g8:256 * g8 + 256], x[:, 0:256], AF.Copy, [xk, "gm"], ["xb%d" % g8], scale=T.gm[:, g8:g8 + 1])

    spread_x(T.xx0, "xc0")
    ms(T.kmin[:], -0.0625, ["kmin"])
    ms(T.k01[:], 1.0, ["k01"])
    ms(T.fl1[:], 0.0, ["fl1"])
    ms(T.fat[:], 0.0, ["fat"])
    ms(T.fbt[:], 0.0, ["fbt"])
    ms(T.nt[:], 0.0, ["nt"])
    ms(T.kmin[:, 0::16], 8192.0, ["kmin"])
    ms(T.k01[:, 0::16], 0.0, ["k01"])
    ms(T.fl1[:, :, 4], 1.0, ["fl1"])
    ms(T.fat[:, :, 6:9], -0.5, ["fat"])
    ms(T.fbt[:, :, 3:6], -0.5, ["fbt"])
    ms(T.fk[:], 0.0, ["fk"])
    ms(T.c256[:], 256.0, ["c256"])
    ms(T.zb[:], 0.0, ["zb"])
    ms(T.col[:, 7:8], -15.5, ["colE"])
    ms(T.col[:, 8:9], -8.0, ["colF"])
    cp(T.p4[:, :, 3], B["S2"][:, 0:16], [], ["dd"], ["S2"])
    cp(T.cc[:], B["S2"][:, 0:16], [], ["cc"], ["S2"])
    for s in range(3):
        ts(T.th3[:, :, s], B["S1"][:, 0:16], 1.0 / 32, A.mult, [], ["th3"], b=["S1"])
    ts(T.thb[:], B["S1"][:, 0:16], 1.0 / 32, A.mult, [], ["thb"], b=["S1"])
    ts(T.th1[:], B["S1"][:, 0:16], 1.0 / 32, A.mult, [], ["th1"], 1.0, A.add, b=["S1"])
    ts(T.nih[:], T.idb[:], -1.0, A.mult, ["idb"], ["nih"])
    cp(T.idh[:], T.idb[:], ["idb"], ["idh"])
    act(T.id8[:], T.idb[:], AF.Copy, ["idb"], ["id8"], scale=-8.0)
    tt(T.coef[:, 0:1], T.z16[:, 17:18], T.z16[:, 16:17], A.subtract, ["z1"], ["cf0"])
    tt(T.coef[:, 1:2], T.z16[:, 17:18], T.z16[:, 18:19], A.subtract, ["z1"], ["cf1"])
    ts(T.sel0[:], T.gm[:], T.z16[:, 18:19], A.mult, ["z1", "gm"], ["sel0"])
    tt(T.thp[:], T.fl1[:, :, 2:5], T.th3[:], A.mult, ["fl1", "th3"], ["thp"])
    for g8 in range(8):
        ts(T.selr[:, g8, :], T.z16[:, 16:19], T.gm[:, g8:g8 + 1], A.mult, ["z1", "gm"], ["selr"])
    ms(T.nt2[:], 0.0, ["nt2"])
    cp(T.cu[:], T.sfw[:].indirect(T.udd[:]), ["sf", "udd"], ["cu"])
    cp(T.sff[:], T.sfw[:], ["sf"], ["sff"])
    PW = []
    for k in range(4):
        c, m = 1024 * k, 1024 * k + (768 if k < 3 else 512)
        ts(T.pw2[:, 2 * c + 1:2 * c + 2048:2], T.pwn[:, c:c + 1024], -1.0, A.mult, ["pw%d" % k], ["pa%d" % k])
        act(T.pw2[:, 2 * c:2 * m:2], T.pwn[:, c:m], AF.Copy, ["pw%d" % k], ["pb%d" % k])
        cp(T.pw2[:, 2 * m:2 * c + 2048:2], T.pwn[:, m:c + 1024], ["pw%d" % k], ["pc%d" % k])
        PW += ["pa%d" % k, "pb%d" % k, "pc%d" % k]
    LLK = ["LL0", "LL1", "LL2"]

    def blockers(av, ak, part):
        nb = B["S1"]
        if part != 1:
            mm(nb[:, 0:16], T.idb[:], T.zb[:, 0:16], True, False, ["zb"], ["S1"])
            mm(nb[:, 0:8], T.id8[:], av(0, 8), False, False, ["id8", ak[0]], ["S1"])
            for g8 in GORDER:
                mm(nb[:, g8:g8 + 1], T.eq[:, g8, 0, :], av(g8, g8 + 1), False, False, ["eq%d" % g8], ["S1"])
                mm(nb[:, 8 + g8:9 + g8], T.eq[:, g8, 1, :], av(g8, g8 + 1), False, False, ["eq%d" % g8, ak[0]], ["S1"])
        if part != 0:
            mm(nb[:, 8:16], T.id8[:], av(8, 16), False, False, [ak[1]], ["S1"])
            for g8 in GORDER:
                mm(nb[:, 8 + g8:9 + g8], T.eq[:, g8, 2, :], av(8 + g8, 9 + g8), False, g8 == 7, ["eq%d" % g8, ak[1]], ["S1"])

    def write_offsets(between=None):
        ts(T.zz[:], B["S1"][:, 0:16], -8.0, A.is_equal, [], ["zz"], b=["S1"])
        if between:
            between()
        tt(T.xso[:].indirect(XL), T.zz[:], T.df[:], A.mult, ["zz", "df"], ["xso"])
        conv("S2", 0, "xso", True)

    def take_offsets():
        ts(T.uso[:], B["S2"][:, 0:16], float(FF), A.add, [], ["uso"], b=["S2"])

    def values():
        act(T.nn[:], B["NB"][:, 0:256], AF.Copy, [], ["nn"], ["NB"])

    def values_new(nt, idm):
        mm(B["NB"][:, 0:256], T[idm][:], T.r3[:], True, False, ["r3", "idh", idm], ["NB"])
        for h in range(2):
            mm(B["NB"][:, 128 * h:128 * h + 128], T[nt][:, 8 * h:8 * h + 8, :], T.idh[:], False, h == 1, [nt], ["NB"])

    def epoch_v():
        ts(T.dig[:, :, 0], T.ff[:], 15, A.bitwise_and, ["ff"], ["dg0"])
        ts(T.dig[:, :, 1], T.ff[:], 4, A.arith_shift_right, ["ff"], ["dg1"], 15, A.bitwise_and)
        ts(T.dig[:, :, 2], T.ff[:], 8, A.arith_shift_right, ["ff"], ["dg2"])
        cp(T.fat[:, :, 0:3], T.dig[:], ["dg0", "dg1", "dg2", "fat"], ["fa0"])

    def epoch_squares():
        act(T.fbt[:, :, 0:3], T.fat[:, :, 0:3], AF.Copy, ["fa0", "fbt"], ["fb0"])
        act(T.fat[:, :, 3:6], T.fat[:, :, 0:3], AF.Square, ["fa0"], ["fa1"])
        act(T.fbt[:, :, 6:9], T.fat[:, :, 0:3], AF.Square, ["fa0"], ["fb1"])

    def epoch_features():
        for h in range(2):
            mm(B["EA"][:, 128 * h:128 * h + 128], T.fat[:, 8 * h:8 * h + 8, :], T.idb[:], True, True, ["fa0", "fa1"], ["EA"])
        for h in range(2):
            mm(B["EB"][:, 128 * h:128 * h + 128], T.fbt[:, 8 * h:8 * h + 8, :], T.idb[:], True, True, ["fb0", "fb1"], ["EB"])
        act(T.fan[:], B["EA"][:, 0:256], AF.Copy, [], ["fan"], ["EA"])
        act(T.fbn[:], B["EB"][:, 0:256], AF.Copy, [], ["fbn"], ["EB"])
        act(T.fao[:], B["EA"][:, 0:256], AF.Copy, ["colB"], ["fao"], ["EA"], scale=T.col[:, 4:5])

    def epoch_pairs(n0, n1):
        for n in range(n0, n1):
            g8 = GORDER[n]
            bk = "EB" if n % 2 == 0 else "EA"
            p0 = 32 * (g8 // 2)
            p1 = p0 + (32 if g8 % 2 else 16)
            fa = "fao" if g8 % 2 else "fan"
            mm(B[bk][:, 0:256], T[fa][p0:p1, 0:128], T.fbn[p0:p1, 0:256], True, True, [fa, "fbn"], [bk])
            mm(B[bk][:, 256:384], T[fa][p0:p1, 128:256], T.fbn[p0:p1, 128:256], True, True, [fa, "fbn"], [bk])
            act(T.eq[:, g8, :, :], B[bk][:, 0:384], AF.Relu, ["onf"], ["eq%d" % g8], [bk], bias=T.onf[:, 0:1], scale=2.0)
            op("G", lambda e, v=T.eq[:, g8, 0::2, :]: e.affine_select(v, v, [[0, 2], [1, 128]], A.is_gt, 0.0, 0, -1),
               ["eq%d" % g8], ["eq%d" % g8])

    def request_sums(xc, xk):
        for r in range(NR):
            for h in range(2):
                c0 = 128 + 32 * r + 16 * h
                mm(B["S1"][:, c0:c0 + 16], xc[:, 128 * h:128 * h + 128], T.hwb[:, r, :, :], True, True, [xk, "hwb"], ["S1"])

    def request():
        ts(T.fj[:], T.ff[:], 3, A.bitwise_and, ["ff"], ["fj"])
        for r in range(NR):
            ts(T.oh[:, 16 * r:16 * r + 16], T.fj[:], float(r), A.is_equal, ["fj"], ["oh"])
        cp(T.hr[:], T.fj[:], ["fj"], ["hr"])
        tt(T.ua[:], B["S1"][:, 128:256:2], T.oh[:], A.mult, ["oh"], ["ua"], ["S1"])
        tt(T.ub[:], B["S1"][:, 129:256:2], T.ua[:], A.mult, ["ua"], ["ub"], ["S1"])
        tt(T.ua[:, 0:32], T.ub[:, 0:32], T.ub[:, 32:64], A.add, ["ub"], ["ua"])
        tt(T.fi[:], T.ua[:, 0:16], T.ua[:, 16:32], A.add, ["ua"], ["fi"])
        ts(T.fj[:], T.fi[:], 5, A.arith_shift_right, ["fi"], ["fj"], FF - 1, A.bitwise_and)
        cp(T.xhh[:].indirect(XL), T.fj[:], ["fj"], ["xhh"])

    def request_send(rnd):
        rq = T["rq%d" % rnd]
        cp(rq[:, 0:16], B["S2"][:, 16:32], [], ["rqo%d" % rnd], ["S2"])
        remote([RemoteDMATransfer(dst_ids=[dst[r] for r in peers], dma_engine_mask=bits(eng), remote_sem=T.sem["rqin%d" % rnd],
                                  srcs=[rq[:, 0:16]], dsts=[rq[:, 16 * s:16 * s + 16] for s in range(1, NR)])], ne, ["rqo%d" % rnd])
        arrive("rqin%d" % rnd, 3 * ne, ["rqi%d" % rnd])

    def answer(rnd):
        rq, ro, rp = T["rq%d" % rnd], T["ro%d" % rnd], T["rp%d" % rnd]
        win = T.LL[:, 0:FF]
        for c in (2, 3, 4):
            cp(T.rg[:, 128 * c:128 * c + 128], win.indirect(rq[:, 8 * c:8 * c + 8]), LLK + ["rqi%d" % rnd], ["rg%d" % c])
            act(T.rg[:, 128 * c + 384:128 * c + 512], win.indirect(rq[:, 8 * c + 24:8 * c + 32]), AF.Copy,
                LLK + ["rqi%d" % rnd], ["rg%d" % (c + 3)])
        for c in (2, 5, 3, 6, 4, 7):
            mm(B["EA"][:, 8 * c:8 * c + 8], T.rg[:, 128 * c:128 * c + 128], T.sel0[:], True, True, ["rg%d" % c, "sel0"], ["EA"])
        act(ro[:], B["EA"][:, 16:64], AF.Copy, [], ["ro%d" % rnd], ["EA"])
        remote([RemoteDMATransfer(dst_ids=[dst[(me - s) % NR]], dma_engine_mask=bits(share[s - 1]), remote_sem=T.sem["rpin%d" % rnd],
                                  src=ro[:, 16 * s - 16:16 * s], dst=rp[:, 16 * me:16 * me + 16]) for s in range(1, NR)],
               ne, ["ro%d" % rnd])
        arrive("rpin%d" % rnd, ne, ["rpi%d" % rnd])
        act(T.rg[:, 0:256], win.indirect(rq[:, 0:16]), AF.Copy, LLK + ["rqo%d" % rnd], ["rg0"])

    def answer_own(rnd):
        for c in range(2):
            mm(B["EB"][:, 8 * c:8 * c + 8], T.rg[:, 128 * c:128 * c + 128], T.sel0[:], True, True, ["rg0"], ["EB"])
        act(T["rp%d" % rnd][:, 16 * me:16 * me + 16], B["EB"][:, 0:16], AF.Copy, [], ["rpo%d" % rnd], ["EB"])

    def planes(q, a, b):
        if a < b:
            src, w = T.pw2[:].indirect(T.cu[:, a:b]), ["G%d" % p for p in range(a, b)]
            if q == "V":
                cp(T.gg[:, 16 * a:16 * b], src, PW + ["cu"], w)
            else:
                act(T.gg[:, 16 * a:16 * b], src, AF.Copy, PW + ["cu"], w)

    XB = ["xb%d" % i for i in range(8)]

    def dots(a, b):
        for p in range(a, b):
            h, qd, n = p // 128, (p % 128) // 32, p % 32
            mm(B["V%d" % h][32 * qd:32 * qd + 16, n:256:32], T.gg[:, 16 * p:16 * p + 16], T.xb[:, p::256], True, True,
               ["G%d" % p] + XB, ["V%d" % h])

    WW = T.ww[:, :, 0:16]
    MS = B["CT"][:, 256:384]
    CNT = T.cn[:, 15::16]

    def test(h, fl, fk, swaps):
        op("V", lambda e: e.transpose(T.ww[:], B["V%d" % h][:, 0:256]), [], ["ww"], ["V%d" % h])
        ts(T.ge[:], WW, 0.0, A.is_ge, ["ww"], ["ge"], 1.0 / 32, A.mult)
        if h:
            act(T.wc[:], WW, AF.Copy, ["ww"], ["wc"])
        else:
            cp(T.wc[:], WW, ["ww"], ["wc"])
        scan(T.cn[:, 128 * h:128 * h + 128], T.k01[:], T.ge[:], A.mult, A.add, ["ge", "k01"], ["cn%d" % h])
        c, cnt = slice(8 * h, 8 * h + 8), T.cn[:, 128 * h + 15:128 * h + 128:16]
        scan(MS, T.kmin[:], T.wc[:], A.add, A.min, ["wc", "kmin"], ["ms"], ["CT"])
        if swaps:
            tt(fl[:, c, 0], cnt, T.tha[:, c], A.is_ge, ["cn%d" % h, "tha"], [fk + "a%d" % h])
        if not h:
            least_b()
        tt(fl[:, c, 4], cnt, T.thb[:, c], A.is_ge, ["cn%d" % h, "thb"], [fk + "b%d" % h])

    def least_b():
        tt(T.nu[:], MS, T.wc[:], A.not_equal, ["ms", "wc"], ["nu"], ["CT"])

    def least_c(h):
        scan(T.mx[:, 128 * h:128 * h + 128], T.nu[:], B["CT"][:, 128 * h:128 * h + 128], A.mult, A.max, ["nu"], ["mx%d" % h], ["CT"])

    def weave(fns):
        segs = []
        for fn in fns:
            n = len(ops)
            fn()
            segs.append(ops[n:])
            del ops[n:]
        for k in range(max([len(x) for x in segs] + [0])):
            ops.extend(x[k] for x in segs if k < len(x))

    first, pending = [], []
    NT = NSUB * NROUND
    for t in range(NT):
        rnd, last_sub, end = t // NSUB, t % NSUB == NSUB - 1, t == NT - 1
        fk, fok = "fl%d" % (t % 2), "fl%d" % (1 - t % 2)
        fl, fo = T[fk], T[fok]
        FK, FOK = [[k, k + "b0", k + "b1"] for k in (fk, fok)]
        xc, xn = T["xx%d" % (t % 2)], T["xx%d" % (1 - t % 2)]
        xck, xnk, xk1 = "xc%d" % (t % 2), "xc%d" % (1 - t % 2), "xn%d" % (t % 2)
        swaps = t >= 2
        epoch = swaps and t % 2 == 0
        kind = ("first", "second")[t] if t < 2 else "req" if last_sub else "plain" if not epoch else "epoch" if t % NSUB else "afterx"
        a0, a1 = SPLIT[kind]
        a1 += 128
        if t:
            cp(T.cu[:], T.sfw[:].indirect(T.udd[:]), ["sf", "udd"], ["cu"])
        act(T.cf[:], T.sff[:].indirect(T.udd[:]), AF.Identity, ["sff", "udd", "colC"], ["cf"], bias=T.col[:, 5:6])
        if kind == "afterx":
            values()
            write_offsets()
        if last_sub:
            request_sums(xc, xck)
        if epoch:
            epoch_pairs(EARLY if kind == "afterx" else 0, 8)
        mm(B["EB"][:, 0:256], T.idb[:], xc[:, 0:256], True, False, [xck], ["EB"])
        mm(B["EB"][:, 0:256], T.idb[:], T.drs[:], False, True, ["dr"], ["EB"])
        planes("S", a0, 128)
        m1 = (a1 + 256) // 4 * 2
        m2 = (m1 + 256) // 4 * 2
        m3 = (m2 + 256) // 4 * 2
        for a, b in ((a1, m1), (m1, m2), (m2, m3), (m3, 256)):
            planes("S", a, b)
        planes("V", 0, a0 // 2)
        for h in range(2):
            op("P", lambda e, h=h: e.transpose(B["CT"][:, 128 * h:128 * h + 128], T.cf[:, 128 * h:128 * h + 128], T.idf[:]),
               ["cf"], [], ["CT"])
        dots(0, a0 // 2)
        if t == 0:
            cp(T.otf[0:96, :], T.oti[0:96, :], ["oti0", "oti1", "oti2"], ["otf"])
            for k in range(3):
                dma("Y", T.LL[2 - k::16, 0:FF], T.otf[32 * k:32 * k + 32, :], r=["otf", "LLz"], w=["LL%d" % k])
        if t == 1:
            ts(T.col[:, 6:7], T.z16[:, 16:17], -1.0, A.mult, ["z1"], ["colD"], 1.0, A.add)
            for g8 in range(8):
                ts(T.seld[:, g8, :], T.coef[:], T.gm[:, g8:g8 + 1], A.mult, ["cf0", "cf1"], ["seld"])
            ts(T.idm[:], T.idb[:], T.col[:, 6:7], A.mult, ["colD"], ["idm"])
            for g8 in range(8):
                ts(T.hwb[:, :, g8, :], T.hwa[:, :, 0:2], T.gm[:, g8:g8 + 1], A.mult, ["hwo", "hwr", "gm"], ["hwb"])
        if last_sub:
            pending.append(request)
        for fn in first:
            fn()
        weave(pending)
        del first[:], pending[:]
        dots(a0, 128)
        if last_sub:
            conv("S2", 16, "xhh")
        planes("V", a0 // 2, a0)
        if last_sub:
            request_send(rnd)
        planes("V", 128, a1)
        dots(a0 // 2, a0)
        if swaps:
            values_new("nt", "idh")
        dots(128, 256)
        act(T.sg[:], B["EB"][:, 0:256], AF.Sign, ["colE"], ["sg"], ["EB"], bias=T.col[:, 7:8])
        test(0, fl, fk, swaps)
        least_c(0)
        av = lambda a, b, fl=fl: fl[:, a:b, 0]
        if swaps:
            blockers(av, [fk + "a0", fk + "a1"], 0)
        test(1, fl, fk, swaps)
        if swaps:
            values()
            blockers(av, [fk + "a0", fk + "a1"], 1)
        least_b()
        tt(T.xxo[:].indirect(XL), fl[:, :, 4], T.c256[:], A.mult, FK[1:] + ["c256"], ["xxo"])
        conv("V1", 256, "xxo", True)
        if swaps:
            write_offsets(lambda: least_c(1))
        else:
            least_c(1)
        mm(B["EA"][:, 0:256], T.idb[:], xc[:, 0:256], True, False, [xck], ["EA"])
        mm(B["EA"][:, 0:256], T.idb[:], T.drs[:], False, False, [], ["EA"])
        mm(B["EA"][:, 0:256], T.id8[:], T.sg[:], False, True, ["sg", "id8"], ["EA"])
        act(xc[:, 256:512], B["EA"][:, 0:256], AF.Identity, ["colF"], [xk1], ["EA"], bias=T.col[:, 8:9])
        if last_sub:
            cp(T.uxo[:], B["V1"][:, 256:272], [], ["uxo"], ["V1"])

        def rows(s0, s1):
            for s in range(s0, s1):
                tt(fl[:, :, 1 + s], CNT, T.thp[:, :, s], A.is_lt, ["cn0", "cn1", "thp"], [fk])

        def new_f():
            tt(T.fi[:], T.mx[:, 15::16], fo[:, :, 4], A.mult, ["mx0", "mx1"] + FOK, ["fi"])
            if last_sub:
                rows(1, 2)
            else:
                cp(T.uxo[:], B["V1"][:, 256:272], [], ["uxo"], ["V1"])
            ts(T.fj[:], T.fi[:], 8191, A.bitwise_and, ["fi"], ["fj"], 1, A.arith_shift_right)
            rows(0, 1)
            tt(T.ff[:], T.fj[:], T.fk[:], A.add, ["fj", "fk"], ["ff"])
            if last_sub:
                rows(2, 3)
            elif swaps:
                take_offsets()
            cp(T.xro[:].indirect(XL), T.ff[:], ["ff"], ["xro"])
            conv("V0", 256, "xro")

        if last_sub:
            take_offsets()
        else:
            new_f()
        if swaps:
            cp(T.LL[:].indirect(T.uso[:]), T.nn[:], ["nn", "uso"], LLK)
        if last_sub:
            answer(rnd)
            new_f()
            answer_own(rnd)
        if end:
            act(T.xf[:], xc[:].indirect(T.uxo[:]), AF.Copy, [xck, xk1, "uxo"], ["xf"])
            for k in range(2):
                dma("Y", T.yt[k::3, :], T.LL[2 - k::16, 0:FF], r=LLK)
            dma("Y", T.yx[:], T.xf[:], r=["xf"])
        else:
            act(xn[:, 0:256], xc[:].indirect(T.uxo[:]), AF.Copy, [xck, xk1, "uxo"], [xnk])
            if not last_sub:
                spread_x(xn, xnk)
            mm(B["S1"][:, 16:64], T.idb[:], T.zb[:, 0:48], True, False, ["zb"], ["S1"])
            for s in range(3):
                mm(B["S1"][:, 16 + s:64:3], T.nih[:], T.p4[:, :, 3], False, False, ["nih", "dd"], ["S1"])
        if last_sub:
            tt(T.p2[:], fl[:, :, 1:4:2], fl[:, :, 2:5:2], A.add, FK, ["p2"])
            tt(T.t1[:], T.p2[:, :, 0], T.p2[:, :, 1], A.add, ["p2"], ["t1"])
        cp(T.uro[:], B["V0"][:, 256:272], [], ["uro"], ["V0"])
        cp(T.r3[:], T.LL[:, 0:FF].indirect(T.uro[:]), LLK + ["uro"], ["r3"])
        if not end:
            for h in range(2):
                mm(B["S1"][:, 16 + 24 * h:40 + 24 * h], T.r3[:, 128 * h:128 * h + 128], T.selr[:], False, h == 1, ["r3", "selr"], ["S1"])
        if not last_sub:
            rows(1, 3)
        else:
            ts(T.t2[:], T.t1[:], 8.0, A.mult, ["t1"], ["t2"])
            tt(T.t1[:], T.t2[:], T.hr[:], A.add, ["t2", "hr"], ["t1"])
            for r in range(NR):
                ts(T.wh[:, 16 * r:16 * r + 16], T.t1[:], float(r), A.is_equal, ["t1"], ["wh"])
        if not end:
            tt(T.p4[:, :, 0:3], B["S1"][:, 16:64], fl[:, :, 1:4], A.mult, FK, ["p4"], ["S1"])
            tt(T.a2[:], T.p4[:, :, 0:2], T.p4[:, :, 2:4], A.add, ["p4", "dd"], ["a2"])

        def flags_a(fl=fl, FK=FK):
            tt(T.p2[:], fl[:, :, 1:4:2], fl[:, :, 2:5:2], A.add, FK, ["p2"])
            tt(T.t2[:], fl[:, :, 4], T.ff[:], A.mult, FK + ["ff"], ["t2"])

        def flags_b(fl=fl, FK=FK):
            tt(T.tha[:], T.th1[:], T.p2[:, :, 0], A.subtract, ["th1", "p2"], ["tha"])
            tt(T.thp[:], fl[:, :, 2:5], T.th3[:], A.mult, FK, ["thp"])
            tt(T.thb[:], T.tha[:], T.p2[:, :, 1], A.subtract, ["tha", "p2"], ["thb"])

        def deltas():
            for h in range(2):
                mm(B["S1"][:, 64 + 16 * h:80 + 16 * h], T.r3[:, 128 * h:128 * h + 128], T.seld[:], True, True, ["r3", "seld"], ["S1"])

        def book(fl=fl, FK=FK, t=t):
            tt(T.fk[:], T.ff[:], T.t2[:], A.subtract, ["ff", "t2"], ["fk"])
            if t >= 1:
                tt(T.nt[:, :, 0:3:2], B["S1"][:, 64:96], fl[:, :, 1:3], A.mult, FK, ["nt"], ["S1"])
                tt(T.t1[:], T.nt[:, :, 0], T.nt[:, :, 2], A.add, ["nt"], ["t1"])
                ts(T.nt[:, :, 1], T.t1[:], -1.0, A.mult, ["t1"], ["nt"])

        def cells(fl=fl, FK=FK):
            tt(T.zz[:], T.p4[:, :, 3], T.cc[:], A.subtract, ["dd", "cc"], ["zz"])
            tt(T.df[:], T.ff[:], T.dmt[:], A.subtract, ["ff", "dmt"], ["df"])
            tt(T.dk[:], T.zz[:], fl[:, :, 4], A.mult, ["zz"] + FK, ["dk"])
            tt(T.cc[:], T.cc[:], T.dk[:], A.add, ["cc", "dk"], ["cc"])

        if not last_sub:
            tt(T.xdd[:].indirect(XL), T.a2[:, :, 0], T.a2[:, :, 1], A.add, ["a2"], ["xdd"])
            conv("S2", 0, "xdd")
            if t >= 1:
                deltas()
            tt(T.p4[:, :, 3], T.a2[:, :, 0], T.a2[:, :, 1], A.add, ["a2"], ["dd"])
            if t % 2:
                epoch_v()
                epoch_squares()
                epoch_features()
                first.append(flags_a)
            else:
                flags_a()
            cp(T.udd[:], B["S2"][:, 0:16], [], ["udd"], ["S2"])
            pending.extend([flags_b, book, cells])
            continue
        rp = T["rp%d" % rnd]
        mm(B["S1"][:, 128:192], T.trp[:], T.wh[:], True, False, ["wh", "trp"], ["S1"])
        for r in range(NR):
            mm(B["S1"][:, 136 + 16 * r:144 + 16 * r], T.onb[:], T.wh[:, 16 * r:16 * r + 8], False, r == NR - 1, ["wh", "onb"], ["S1"])
        if not end:
            tt(T.p4[:, :, 3], T.a2[:, :, 0], T.a2[:, :, 1], A.add, ["a2"], ["dd"])
            epoch_v()
            epoch_squares()
            spread_x(xn, xnk)
            epoch_features()
        ts(T.ua[:], B["S1"][:, 128:192], 32.0, A.is_lt, [], ["ua"], b=["S1"])
        tt(T.osv[:], T.ua[:], T.wh[:], A.mult, ["ua", "wh"], ["osv"])
        tt(T.ua[:, 0:32], T.osv[:, 0:32], T.osv[:, 32:64], A.add, ["osv"], ["ua"])
        tt(T.srv[:], T.ua[:, 0:16], T.ua[:, 16:32], A.add, ["ua"], ["srv"])
        blockers(lambda a, b: T.srv[:, a:b], ["srv", "srv"], 2)
        cells()
        if end:
            cp(T.xro[:].indirect(XL), T.cc[:], ["cc"], ["xro"])
            write_offsets()
            conv("V0", 256, "xro")
            take_offsets()
            cp(T.ycf[:], B["V0"][:, 256:272], [], ["ycf"], ["V0"])
            dma("Y", T.yc[:], T.ycf[:], r=["ycf"])
        else:
            tt(T.t1[:], T.srv[:], T.p4[:, :, 3], A.mult, ["srv", "dd"], ["t1"])
            tt(fl[:, :, 1], fl[:, :, 1], T.srv[:], A.add, FK + ["srv"], [fk])
            tt(T.dk[:], T.p4[:, :, 3], T.t1[:], A.subtract, ["t1", "dd"], ["dk"])
            epoch_pairs(0, EARLY)
            flags_a()
            flags_b()
        tt(T.ub[:], rp[:], T.osv[:], A.mult, ["rpi%d" % rnd, "rpo%d" % rnd, "osv"], ["ub"])
        tt(T.ua[:, 0:32], T.ub[:, 0:32], T.ub[:, 32:64], A.add, ["ub"], ["ua"])
        if not end:
            tt(T.ans[:], T.ua[:, 0:16], T.ua[:, 16:32], A.add, ["ua"], ["ans"])
            tt(T.xdd[:].indirect(XL), T.ans[:], T.dk[:], A.add, ["ans", "dk"], ["xdd"])
            conv("S2", 32, "xdd")
        tt(T.nt2[:, :, 0], T.ua[:, 0:16], T.ua[:, 16:32], A.add, ["ua"], ["nt2"])
        values_new("nt2", "idm")
        if end:
            cp(T.nn[:], B["NB"][:, 0:256], [], ["nn"], ["NB"])
            cp(T.LL[:].indirect(T.uso[:]), T.nn[:], ["nn", "uso"], LLK)
            dma("Y", T.yt[2::3, :], T.LL[0::16, 0:FF], r=LLK)
            break
        tt(T.p4[:, :, 3], T.ans[:], T.dk[:], A.add, ["ans", "dk"], ["dd"])
        cp(T.udd[:], B["S2"][:, 32:48], [], ["udd"], ["S2"])

        def rewrite(deltas=deltas):
            take_offsets()
            cp(T.LL[:].indirect(T.uso[:]), T.nn[:], ["nn", "uso"], LLK)
            cp(T.r3[:], T.LL[:, 0:FF].indirect(T.uro[:]), LLK + ["uro"], ["r3"])
            deltas()

        first.append(rewrite)
        pending.append(book)
    emit(g, T, ops)
